import numpy as np
import ml_dtypes


def mxq(x, axis, fmt="e4m3"):
    dtype, down = {"e4m3": (ml_dtypes.float8_e4m3fn, 7), "e5m2": (ml_dtypes.float8_e5m2, 14)}[fmt]
    v = np.moveaxis(np.asarray(x, np.float32).astype(ml_dtypes.bfloat16).astype(np.float64), axis, -1)
    blocks = v.reshape(v.shape[:-1] + (-1, 32))
    amax = np.abs(blocks).max(-1, keepdims=True)
    byte = np.maximum(np.where(amax > 0, np.frexp(amax)[1] - 1 + 127, 0) - down, 1)
    scale = np.exp2(byte - 127.0)
    codes = (blocks / scale).astype(np.float32).astype(dtype).astype(np.float64)
    return np.moveaxis((codes * scale).reshape(v.shape), -1, axis)


WIDE = False


def mx_kscale(k):
    if not WIDE:
        return np.ones(k)
    levels = np.array([10, -10, 5, -5, 0])
    if k % 512:
        return np.exp2(np.random.permutation(np.resize(levels, k // 32))).repeat(32)
    a = np.empty((k // 512, 16))
    for p in range(k // 512):
        a[p, :8] = np.random.permutation(np.resize(levels, 8))
        for g in range(8):
            far = levels[np.abs(levels - a[p, g]) >= 10]
            a[p, g + 8] = far[np.random.randint(len(far))]
    return np.exp2(a.ravel()).repeat(32)


def f64(x):
    return np.asarray(x).astype(np.float64)


def striped(idx):
    return np.tile(idx.reshape(-1, 16).T, (8, 1)).astype(np.uint16)


def unstriped(offs):
    return offs[:16].T.reshape(-1).astype(np.int64)


def pack_weight(w):
    k, n = w.shape
    w = f64(np.asarray(w, np.float32).astype(ml_dtypes.bfloat16)).reshape(k // 32, 32, n)
    amax = np.abs(w).max(1)
    byte = np.clip(np.where(amax > 0, np.frexp(amax)[1] - 1 + 127 - 7, 1), 1, 254)
    scaled = (w * np.exp2(127.0 - byte)[:, None, :]).reshape(k, n).astype(np.float32)
    words = np.ascontiguousarray(scaled.reshape(k // 512, 128, 4, n).transpose(0, 1, 3, 2)).astype(ml_dtypes.float8_e4m3fn).view(np.uint8)
    return words, np.ascontiguousarray(byte.astype(np.uint8).reshape(k // 512, 16, n))


def unpack_weight(words, scales):
    g, p, n, _ = words.shape
    vals = np.ascontiguousarray(words).view(ml_dtypes.float8_e4m3fn).astype(np.float64) * np.repeat(np.exp2(scales.astype(np.float64) - 127.0), 8, axis=1)[..., None]
    return vals.transpose(0, 1, 3, 2).reshape(g * 512, n)


K, T, S, H, N = 1024, 2048, 1024, 512, 128


def setup_inputs():
    n = np.random.standard_normal
    s = mx_kscale(K)[:, None]
    u = mx_kscale(H)
    packed_w2 = pack_weight(n((H, N)) / np.sqrt(H) / u[:, None])
    return {
        "xT": (n((K, T)) * s).astype(np.float32),
        "w1": (n((K, H)) / np.sqrt(K) / s * u).astype(np.float32),
        "w2_words": packed_w2[0],
        "w2_scales": packed_w2[1],
        "offs": striped(np.random.permutation(T)[:S]),
    }


def reference(xT, w1, w2_words, w2_scales, offs):
    xq = mxq(f64(xT)[:, unstriped(offs)], 0, "e4m3")
    h = mxq(f64(w1), 0, "e4m3").T @ xq
    z = h - h.mean(axis=1, keepdims=True)
    return unpack_weight(w2_words, w2_scales).T @ mxq(z, 0, "e4m3")

@@ -1,0 +1,219 @@
+from contextlib import ExitStack
+
+import concourse.mybir as mybir
+
+K, T, S, H, N = 1024, 2048, 1024, 512, 128
+FLOPS = 2 * K * H * S + 2 * H * N * S
+
+F32 = mybir.dt.float32
+BF16 = mybir.dt.bfloat16
+I32 = mybir.dt.int32
+U32 = mybir.dt.uint32
+U16 = mybir.dt.uint16
+U8 = mybir.dt.uint8
+FP8X4 = mybir.dt.float8_e4m3fn_x4
+COPY = mybir.ActivationFunctionType.Copy
+IDENTITY = mybir.ActivationFunctionType.Identity
+ADD = mybir.AluOpType.add
+MULT = mybir.AluOpType.mult
+
+P = 128
+PACK = 4
+PASSES = 2
+HALF = 512
+
+X_CHUNKS = {
+    (0, 0): [(2048, 768)],
+    (0, 1): [(2048, 512)],
+    (1, 0): [(1024, 256), (1024, 256)],
+    (1, 1): [(1024, 256), (512, 128), (512, 352)],
+}
+W0_SCALAR_ROWS = 44
+Z_SLICES = [(256, True), (256, False), (256, False), (128, True), (128, False)]
+
+
+def tile_picked_deepset_none_e_kernel(tc, xT, w1, w2_words, w2_scales, offs, out):
+    nc = tc.nc
+    with ExitStack() as ctx:
+        keep = ctx.enter_context(tc.tile_pool(name="keep", bufs=1))
+        psum = ctx.enter_context(tc.psum_pool(name="psum", bufs=1))
+
+        offsets = keep.tile([P, S // 16], U16, name="offsets")
+        w2_codes = keep.tile([P, N], U32, name="w2_codes", align_bytes=64)
+        w2_plane = keep.tile([P, N], U8, name="w2_plane", align_bytes=64)
+        nc.vector.memset(w2_plane[:].bitcast(I32), 0)
+        nc.gpsimd.dma_start(out=w2_codes[:].bitcast(I32), in_=w2_words[0].rearrange("p n t -> p (n t)").bitcast(I32))
+        for q in range(4):
+            nc.gpsimd.dma_start(out=w2_plane[32 * q : 32 * q + 4, :].bitcast(I32), in_=w2_scales[0, 4 * q : 4 * q + 4, :].bitcast(I32))
+
+        x_rows = xT.rearrange("(g p j) c -> g p j c", g=PASSES, j=PACK)
+        w_rows = w1.rearrange("(g p j) c -> g p j c", g=PASSES, j=PACK)
+
+        x_raw = {}
+        for g in range(PASSES):
+            for u in range(2):
+                c0 = 0
+                for i, (width, share) in enumerate(X_CHUNKS[(g, u)]):
+                    raw = keep.tile([P, 2, width], F32, name="x_raw_%d_%d_%d" % (g, u, i))
+                    nc.sync.dma_start(out=raw[:], in_=x_rows[g][:, 2 * u : 2 * u + 2, c0 : c0 + width])
+                    x_raw[(g, u, i)] = raw
+                    c0 = c0 + width
+                if (g, u) == (0, 0):
+                    nc.sync.dma_start(offsets[:], offs)
+        w0_raw = keep.tile([P, PACK, H], F32, name="w0_raw")
+        nc.sync.dma_start(out=w0_raw[:], in_=w_rows[0])
+        w1_raw = []
+        for u in range(2):
+            raw = keep.tile([P, 2, H], F32, name="w1_raw_%d" % u)
+            nc.sync.dma_start(out=raw[:], in_=w_rows[1][:, 2 * u : 2 * u + 2, :])
+            w1_raw.append(raw)
+
+        def cast(on_vector, dst, src):
+            if on_vector:
+                nc.vector.tensor_copy(out=dst, in_=src)
+            else:
+                nc.scalar.activation(out=dst, in_=src, func=COPY)
+
+        def cast_pair(g, u):
+            pair = keep.tile([P, 2 * T], BF16, name="pair_%d_%d" % (g, u), align_bytes=64)
+            dst = pair[:].rearrange("p (c e) -> p c e", e=2)
+            c0 = 0
+            for i, (width, share) in enumerate(X_CHUNKS[(g, u)]):
+                src = x_raw[(g, u, i)][:].rearrange("p e c -> p c e")
+                cut = width - share
+                cast(False, dst[:, c0 : c0 + cut, :], src[:, 0:cut, :])
+                cast(True, dst[:, c0 + cut : c0 + width, :], src[:, cut:width, :])
+                c0 = c0 + width
+            return pair
+
+        picked = {}
+        for g in range(PASSES):
+            for h in range(2):
+                picked[(g, h)] = keep.tile([P, 2, HALF], U32, name="picked_%d_%d" % (g, h), align_bytes=64)
+
+        def gather(g, u, pair, h):
+            nc.vector.tensor_copy(
+                out=picked[(g, h)][:, u, :],
+                in_=pair[:].bitcast(U32).indirect(offsets[:, h * HALF // 16 : (h + 1) * HALF // 16]),
+            )
+
+        def weave(g, h, on_vector):
+            grouped = keep.tile([P, PACK * HALF], BF16, name="x_grouped_%d_%d" % (g, h), align_bytes=64)
+            if on_vector:
+                nc.vector.tensor_copy(
+                    out=grouped[:].bitcast(I32).rearrange("p (n u) -> p n u", u=2),
+                    in_=picked[(g, h)][:].bitcast(I32).rearrange("p u n -> p n u"),
+                )
+            else:
+                nc.scalar.copy(
+                    out=grouped[:].bitcast(U32).rearrange("p (n u) -> p n u", u=2),
+                    in_=picked[(g, h)][:].rearrange("p u n -> p n u"),
+                )
+            return grouped
+
+        def quantise(name, grouped, width):
+            codes = keep.tile([P, width], U32, name=name + "_codes", align_bytes=64)
+            plane = keep.tile([P, width], U8, name=name + "_plane", align_bytes=64)
+            nc.vector.quantize_mx(out=codes[:].bitcast(FP8X4), scales=plane[:], in_=grouped)
+            return codes, plane
+
+        banks = {}
+        for h in range(2):
+            for t in range(PACK):
+                banks[(t, h)] = psum.tile([P, HALF], F32, name="bank", tag="bank_%d_%d" % (t, h))
+
+        def product(g, h, xq, wq):
+            for t in range(PACK):
+                nc.tensor.matmul_mx(
+                    out=banks[(t, h)][:],
+                    lhsT=wq[t][0][:].bitcast(FP8X4),
+                    lhsT_scale=wq[t][1][:],
+                    rhs=xq[0][:].bitcast(FP8X4),
+                    rhs_scale=xq[1][:],
+                    start=(g == 0),
+                    stop=(g == PASSES - 1),
+                )
+
+        xq = {}
+        for u in range(2):
+            pair = cast_pair(0, u)
+            for h in range(2):
+                gather(0, u, pair, h)
+        grouped = [weave(0, h, True) for h in range(2)]
+        for h in range(2):
+            xq[(0, h)] = quantise("xq_0_%d" % h, grouped[h][:], HALF)
+        for u in range(2):
+            pair = cast_pair(1, u)
+            for h in range(2):
+                gather(1, u, pair, h)
+        grouped0 = weave(1, 0, False)
+
+        w_grouped = [keep.tile([P, PACK * H], BF16, name="w_grouped_%d" % g, align_bytes=64) for g in range(PASSES)]
+        w_dst = [w_grouped[g][:].rearrange("p (t m j) -> p m j t", t=PACK, j=PACK) for g in range(PASSES)]
+        src = w0_raw[:].rearrange("p j (m t) -> p m j t", t=PACK)
+        cast(False, w_dst[0][:, 0:W0_SCALAR_ROWS], src[:, 0:W0_SCALAR_ROWS])
+        cast(True, w_dst[0][:, W0_SCALAR_ROWS:P], src[:, W0_SCALAR_ROWS:P])
+        wq0 = [quantise("wq_0_%d" % t, w_grouped[0][:, t * H : (t + 1) * H], P) for t in range(PACK)]
+        for h in range(2):
+            product(0, h, xq[(0, h)], wq0)
+
+        xq[(1, 0)] = quantise("xq_1_0", grouped0[:], HALF)
+        for u in range(2):
+            src = w1_raw[u][:].rearrange("p j (m t) -> p m j t", t=PACK)
+            cast(u == 1, w_dst[1][:, :, 2 * u : 2 * u + 2, :], src)
+        grouped1 = weave(1, 1, False)
+        wq1 = [quantise("wq_1_%d" % t, w_grouped[1][:, t * H : (t + 1) * H], P) for t in range(PACK)]
+        xq[(1, 1)] = quantise("xq_1_1", grouped1[:], HALF)
+
+        sums = keep.tile([P, 2 * PACK], F32, name="sums")
+        hidden = [keep.tile([P, PACK * HALF], F32, name="hidden_%d" % h) for h in range(2)]
+        for h in range(2):
+            product(1, h, xq[(1, h)], wq1)
+            for t in range(PACK):
+                dst = hidden[h][:, t * HALF : (t + 1) * HALF]
+                total = sums[:, h * PACK + t : h * PACK + t + 1]
+                if t % 2 == 1:
+                    nc.vector.tensor_scalar(out=dst, in0=banks[(t, h)][:], scalar1=1.0, scalar2=None, op0=MULT, op1=ADD, accum_out=total)
+                else:
+                    nc.scalar.activation(out=dst, in_=banks[(t, h)][:], func=COPY, accum_out=total)
+            if h == 0:
+                first_part = keep.tile([P, PACK], F32, name="first_part")
+                nc.vector.tensor_scalar(out=first_part[:], in0=sums[:, 0:PACK], scalar1=-1.0 / S, scalar2=None, op0=MULT)
+        minus_mean = keep.tile([P, PACK], F32, name="minus_mean")
+        nc.vector.scalar_tensor_tensor(
+            out=minus_mean[:], in0=sums[:, PACK : 2 * PACK], scalar=-1.0 / S, in1=first_part[:], op0=MULT, op1=ADD
+        )
+
+        c0 = 0
+        for i, (width, on_vector) in enumerate(Z_SLICES):
+            h, n0 = divmod(c0, HALF)
+            rows = hidden[h][:].rearrange("p (t n) -> p t n", t=PACK)[:, :, n0 : n0 + width]
+            z = keep.tile([P, PACK * width], BF16, name="z_%d" % i, align_bytes=64)
+            z_dst = z[:].rearrange("p (c i t) -> p c t i", i=4, t=PACK)
+            if on_vector:
+                nc.vector.tensor_tensor(
+                    out=z_dst,
+                    in0=rows.rearrange("p t (c i) -> p c t i", i=4),
+                    in1=minus_mean[:].unsqueeze(1).unsqueeze(3).to_broadcast([P, width // 4, PACK, 4]),
+                    op=ADD,
+                )
+            else:
+                z_rows = keep.tile([P, PACK, width], BF16, name="z_rows_%d" % i, align_bytes=64)
+                for t in range(PACK):
+                    nc.scalar.activation(out=z_rows[:, t, :], in_=rows[:, t, :], func=IDENTITY, bias=minus_mean[:, t : t + 1])
+                nc.vector.tensor_copy(out=z_dst, in_=z_rows[:].rearrange("p t (c i) -> p c t i", i=4))
+            zq = quantise("zq_%d" % i, z[:], width)
+            acc = psum.tile([P, HALF], F32, name="acc", tag="bank_%d_%d" % (i % PACK, i // PACK))
+            nc.tensor.matmul_mx(
+                out=acc[:, 0:width],
+                lhsT=w2_codes[:].bitcast(FP8X4),
+                lhsT_scale=w2_plane[:],
+                rhs=zq[0][:].bitcast(FP8X4),
+                rhs_scale=zq[1][:],
+                start=True,
+                stop=True,
+            )
+            result = keep.tile([P, width], F32, name="result_%d" % i)
+            cast(i == len(Z_SLICES) - 1, result[:], acc[:, 0:width])
+            nc.sync.dma_start(out=out[:, c0 : c0 + width], in_=result[:])
+            c0 = c0 + width

@@ -23,13 +23,13 @@ PASSES = 2
 HALF = 512
 
 X_CHUNKS = {
-    (0, 0): [(2048, 768)],
-    (0, 1): [(2048, 512)],
-    (1, 0): [(1024, 256), (1024, 256)],
-    (1, 1): [(1024, 256), (512, 128), (512, 352)],
+    (0, 0): [(0, 1024, 640), (1024, 1024, 640)],
+    (0, 1): [(0, 1280, 512), (1280, 768, 512)],
+    (1, 0): [(0, 1024, 0), (1024, 1024, 704)],
+    (1, 1): [(0, 768, 0), (768, 512, 0), (1280, 512, 512), (1792, 256, 64)],
 }
 W0_SCALAR_ROWS = 44
-Z_SLICES = [(256, True), (256, False), (256, False), (128, True), (128, False)]
+Z_SLICES = [(256, "vector"), (256, "both"), (256, "both"), (128, "scalar"), (128, "vector")]
 
 
 def tile_picked_deepset_none_e_kernel(tc, xT, w1, w2_words, w2_scales, offs, out):
@@ -42,9 +42,6 @@ def tile_picked_deepset_none_e_kernel(tc, xT, w1, w2_words, w2_scales, offs, out
         w2_codes = keep.tile([P, N], U32, name="w2_codes", align_bytes=64)
         w2_plane = keep.tile([P, N], U8, name="w2_plane", align_bytes=64)
         nc.vector.memset(w2_plane[:].bitcast(I32), 0)
-        nc.gpsimd.dma_start(out=w2_codes[:].bitcast(I32), in_=w2_words[0].rearrange("p n t -> p (n t)").bitcast(I32))
-        for q in range(4):
-            nc.gpsimd.dma_start(out=w2_plane[32 * q : 32 * q + 4, :].bitcast(I32), in_=w2_scales[0, 4 * q : 4 * q + 4, :].bitcast(I32))
 
         x_rows = xT.rearrange("(g p j) c -> g p j c", g=PASSES, j=PACK)
         w_rows = w1.rearrange("(g p j) c -> g p j c", g=PASSES, j=PACK)
@@ -52,21 +49,20 @@ def tile_picked_deepset_none_e_kernel(tc, xT, w1, w2_words, w2_scales, offs, out
         x_raw = {}
         for g in range(PASSES):
             for u in range(2):
-                c0 = 0
-                for i, (width, share) in enumerate(X_CHUNKS[(g, u)]):
-                    raw = keep.tile([P, 2, width], F32, name="x_raw_%d_%d_%d" % (g, u, i))
+                for i, (c0, width, share) in enumerate(X_CHUNKS[(g, u)]):
+                    raw = keep.tile([P, 2, width], F32, name="x_raw", tag="x_raw_%d_%d_%d" % (g, u, i), align_bytes=64)
                     nc.sync.dma_start(out=raw[:], in_=x_rows[g][:, 2 * u : 2 * u + 2, c0 : c0 + width])
                     x_raw[(g, u, i)] = raw
-                    c0 = c0 + width
                 if (g, u) == (0, 0):
                     nc.sync.dma_start(offsets[:], offs)
-        w0_raw = keep.tile([P, PACK, H], F32, name="w0_raw")
-        nc.sync.dma_start(out=w0_raw[:], in_=w_rows[0])
-        w1_raw = []
-        for u in range(2):
-            raw = keep.tile([P, 2, H], F32, name="w1_raw_%d" % u)
-            nc.sync.dma_start(out=raw[:], in_=w_rows[1][:, 2 * u : 2 * u + 2, :])
-            w1_raw.append(raw)
+        w_raw = []
+        for g in range(PASSES):
+            raw = keep.tile([P, PACK, H], F32, name="w_raw", tag="w_raw_%d" % g, align_bytes=64)
+            nc.sync.dma_start(out=raw[:], in_=w_rows[g])
+            w_raw.append(raw)
+        nc.sync.dma_start(out=w2_codes[:].bitcast(I32), in_=w2_words[0].rearrange("p n t -> p (n t)").bitcast(I32))
+        for q in range(4):
+            nc.sync.dma_start(out=w2_plane[32 * q : 32 * q + 4, :].bitcast(I32), in_=w2_scales[0, 4 * q : 4 * q + 4, :].bitcast(I32))
 
         def cast(on_vector, dst, src):
             if on_vector:
@@ -74,45 +70,37 @@ def tile_picked_deepset_none_e_kernel(tc, xT, w1, w2_words, w2_scales, offs, out
             else:
                 nc.scalar.activation(out=dst, in_=src, func=COPY)
 
+        pairs = keep.tile([P, 4 * 2 * T], BF16, name="pairs", tag="pairs", align_bytes=64)
+
         def cast_pair(g, u):
-            pair = keep.tile([P, 2 * T], BF16, name="pair_%d_%d" % (g, u), align_bytes=64)
-            dst = pair[:].rearrange("p (c e) -> p c e", e=2)
-            c0 = 0
-            for i, (width, share) in enumerate(X_CHUNKS[(g, u)]):
+            dst = pairs[:, (2 * g + u) * 2 * T : (2 * g + u + 1) * 2 * T].rearrange("p (c e) -> p c e", e=2)
+            for i, (c0, width, share) in enumerate(X_CHUNKS[(g, u)]):
                 src = x_raw[(g, u, i)][:].rearrange("p e c -> p c e")
-                cut = width - share
-                cast(False, dst[:, c0 : c0 + cut, :], src[:, 0:cut, :])
-                cast(True, dst[:, c0 + cut : c0 + width, :], src[:, cut:width, :])
-                c0 = c0 + width
-            return pair
+                if share < width:
+                    cast(False, dst[:, c0 + share : c0 + width, :], src[:, share:width, :])
+                if share > 0:
+                    cast(True, dst[:, c0 : c0 + share, :], src[:, 0:share, :])
 
-        picked = {}
-        for g in range(PASSES):
-            for h in range(2):
-                picked[(g, h)] = keep.tile([P, 2, HALF], U32, name="picked_%d_%d" % (g, h), align_bytes=64)
+        def gather(g, u, picked, n0, width):
+            window = pairs[:].bitcast(U32)[:, (2 * g + u) * T : (2 * g + u + 1) * T]
+            nc.vector.tensor_copy(out=picked[:, u, :], in_=window.indirect(offsets[:, n0 // 16 : (n0 + width) // 16]))
 
-        def gather(g, u, pair, h):
-            nc.vector.tensor_copy(
-                out=picked[(g, h)][:, u, :],
-                in_=pair[:].bitcast(U32).indirect(offsets[:, h * HALF // 16 : (h + 1) * HALF // 16]),
-            )
-
-        def weave(g, h, on_vector):
-            grouped = keep.tile([P, PACK * HALF], BF16, name="x_grouped_%d_%d" % (g, h), align_bytes=64)
+        def weave(picked, width, on_vector, tag):
+            grouped = keep.tile([P, PACK * width], BF16, name="x_grouped", tag=tag, align_bytes=64)
             if on_vector:
                 nc.vector.tensor_copy(
                     out=grouped[:].bitcast(I32).rearrange("p (n u) -> p n u", u=2),
-                    in_=picked[(g, h)][:].bitcast(I32).rearrange("p u n -> p n u"),
+                    in_=picked[:].bitcast(I32).rearrange("p u n -> p n u"),
                 )
             else:
                 nc.scalar.copy(
                     out=grouped[:].bitcast(U32).rearrange("p (n u) -> p n u", u=2),
-                    in_=picked[(g, h)][:].rearrange("p u n -> p n u"),
+                    in_=picked[:].rearrange("p u n -> p n u"),
                 )
             return grouped
 
-        def quantise(name, grouped, width):
-            codes = keep.tile([P, width], U32, name=name + "_codes", align_bytes=64)
+        def quantise(name, grouped, width, tag):
+            codes = keep.tile([P, width], U32, name="codes", tag=tag, align_bytes=64)
             plane = keep.tile([P, width], U8, name=name + "_plane", align_bytes=64)
             nc.vector.quantize_mx(out=codes[:].bitcast(FP8X4), scales=plane[:], in_=grouped)
             return codes, plane
@@ -122,57 +110,62 @@ def tile_picked_deepset_none_e_kernel(tc, xT, w1, w2_words, w2_scales, offs, out
             for t in range(PACK):
                 banks[(t, h)] = psum.tile([P, HALF], F32, name="bank", tag="bank_%d_%d" % (t, h))
 
-        def product(g, h, xq, wq):
+        def product(g, h, xq, cols, wq):
             for t in range(PACK):
                 nc.tensor.matmul_mx(
                     out=banks[(t, h)][:],
-                    lhsT=wq[t][0][:].bitcast(FP8X4),
-                    lhsT_scale=wq[t][1][:],
-                    rhs=xq[0][:].bitcast(FP8X4),
-                    rhs_scale=xq[1][:],
+                    lhsT=wq[0][:, t * P : (t + 1) * P].bitcast(FP8X4),
+                    lhsT_scale=wq[1][:, t * P : (t + 1) * P],
+                    rhs=xq[0][:, cols].bitcast(FP8X4),
+                    rhs_scale=xq[1][:, cols],
                     start=(g == 0),
                     stop=(g == PASSES - 1),
                 )
 
-        xq = {}
+        picked0 = [keep.tile([P, 2, HALF], U32, name="picked", tag="picked_0_%d" % h, align_bytes=64) for h in range(2)]
         for u in range(2):
-            pair = cast_pair(0, u)
+            cast_pair(0, u)
             for h in range(2):
-                gather(0, u, pair, h)
-        grouped = [weave(0, h, True) for h in range(2)]
-        for h in range(2):
-            xq[(0, h)] = quantise("xq_0_%d" % h, grouped[h][:], HALF)
+                gather(0, u, picked0[h], h * HALF, HALF)
+        x_grouped = [weave(picked0[h], HALF, h == 1, "x_grouped_0_%d" % h) for h in range(2)]
+        xq0 = [quantise("xq_0_%d" % h, x_grouped[h][:], HALF, "xq_0_%d" % h) for h in range(2)]
+        picked1 = [keep.tile([P, 2, HALF], U32, name="picked", tag="picked_1_%d" % h, align_bytes=64) for h in range(2)]
         for u in range(2):
-            pair = cast_pair(1, u)
+            cast_pair(1, u)
             for h in range(2):
-                gather(1, u, pair, h)
-        grouped0 = weave(1, 0, False)
+                gather(1, u, picked1[h], h * HALF, HALF)
 
-        w_grouped = [keep.tile([P, PACK * H], BF16, name="w_grouped_%d" % g, align_bytes=64) for g in range(PASSES)]
-        w_dst = [w_grouped[g][:].rearrange("p (t m j) -> p m j t", t=PACK, j=PACK) for g in range(PASSES)]
-        src = w0_raw[:].rearrange("p j (m t) -> p m j t", t=PACK)
-        cast(False, w_dst[0][:, 0:W0_SCALAR_ROWS], src[:, 0:W0_SCALAR_ROWS])
-        cast(True, w_dst[0][:, W0_SCALAR_ROWS:P], src[:, W0_SCALAR_ROWS:P])
-        wq0 = [quantise("wq_0_%d" % t, w_grouped[0][:, t * H : (t + 1) * H], P) for t in range(PACK)]
+        def cast_weights(g):
+            grouped = keep.tile([P, PACK * H], BF16, name="w_grouped", tag="w_grouped_%d" % g, align_bytes=64)
+            src = w_raw[g][:].rearrange("p j (m t) -> p m j t", t=PACK)
+            cast(False, grouped[:].rearrange("p (t m j) -> p m j t", t=PACK, j=PACK), src)
+            return grouped
+
+        def quantise_weights(g, grouped):
+            codes = keep.tile([P, H], U32, name="wq_codes_%d" % g, align_bytes=64)
+            plane = keep.tile([P, H], U8, name="wq_plane_%d" % g, align_bytes=64)
+            for t in range(PACK):
+                cols = slice(t * P, (t + 1) * P)
+                nc.vector.quantize_mx(out=codes[:, cols].bitcast(FP8X4), scales=plane[:, cols], in_=grouped[:, H * t : H * (t + 1)])
+            return codes, plane
+
+        grouped = weave(picked1[0], HALF, True, "x_grouped_1_0")
+        xq1 = [quantise("xq_1_0", grouped[:], HALF, "xq_1_0")]
+        wq0 = quantise_weights(0, cast_weights(0))
         for h in range(2):
-            product(0, h, xq[(0, h)], wq0)
-
-        xq[(1, 0)] = quantise("xq_1_0", grouped0[:], HALF)
-        for u in range(2):
-            src = w1_raw[u][:].rearrange("p j (m t) -> p m j t", t=PACK)
-            cast(u == 1, w_dst[1][:, :, 2 * u : 2 * u + 2, :], src)
-        grouped1 = weave(1, 1, False)
-        wq1 = [quantise("wq_1_%d" % t, w_grouped[1][:, t * H : (t + 1) * H], P) for t in range(PACK)]
-        xq[(1, 1)] = quantise("xq_1_1", grouped1[:], HALF)
+            product(0, h, xq0[h], slice(0, HALF), wq0)
+        grouped = weave(picked1[1], HALF, True, "w_grouped_0")
+        xq1.append(quantise("xq_1_1", grouped[:], HALF, "xq_1_1"))
+        wq1 = quantise_weights(1, cast_weights(1))
 
         sums = keep.tile([P, 2 * PACK], F32, name="sums")
         hidden = [keep.tile([P, PACK * HALF], F32, name="hidden_%d" % h) for h in range(2)]
         for h in range(2):
-            product(1, h, xq[(1, h)], wq1)
+            product(1, h, xq1[h], slice(0, HALF), wq1)
             for t in range(PACK):
                 dst = hidden[h][:, t * HALF : (t + 1) * HALF]
                 total = sums[:, h * PACK + t : h * PACK + t + 1]
-                if t % 2 == 1:
+                if t % 2 == 0:
                     nc.vector.tensor_scalar(out=dst, in0=banks[(t, h)][:], scalar1=1.0, scalar2=None, op0=MULT, op1=ADD, accum_out=total)
                 else:
                     nc.scalar.activation(out=dst, in_=banks[(t, h)][:], func=COPY, accum_out=total)
@@ -180,17 +173,18 @@ def tile_picked_deepset_none_e_kernel(tc, xT, w1, w2_words, w2_scales, offs, out
                 first_part = keep.tile([P, PACK], F32, name="first_part")
                 nc.vector.tensor_scalar(out=first_part[:], in0=sums[:, 0:PACK], scalar1=-1.0 / S, scalar2=None, op0=MULT)
         minus_mean = keep.tile([P, PACK], F32, name="minus_mean")
-        nc.vector.scalar_tensor_tensor(
-            out=minus_mean[:], in0=sums[:, PACK : 2 * PACK], scalar=-1.0 / S, in1=first_part[:], op0=MULT, op1=ADD
-        )
+        for t0, t1 in ((0, PACK - 1), (PACK - 1, PACK)):
+            nc.vector.scalar_tensor_tensor(
+                out=minus_mean[:, t0:t1], in0=sums[:, PACK + t0 : PACK + t1], scalar=-1.0 / S, in1=first_part[:, t0:t1], op0=MULT, op1=ADD
+            )
 
         c0 = 0
-        for i, (width, on_vector) in enumerate(Z_SLICES):
+        for i, (width, route) in enumerate(Z_SLICES):
             h, n0 = divmod(c0, HALF)
             rows = hidden[h][:].rearrange("p (t n) -> p t n", t=PACK)[:, :, n0 : n0 + width]
             z = keep.tile([P, PACK * width], BF16, name="z_%d" % i, align_bytes=64)
             z_dst = z[:].rearrange("p (c i t) -> p c t i", i=4, t=PACK)
-            if on_vector:
+            if route == "vector":
                 nc.vector.tensor_tensor(
                     out=z_dst,
                     in0=rows.rearrange("p t (c i) -> p c t i", i=4),
@@ -201,8 +195,11 @@ def tile_picked_deepset_none_e_kernel(tc, xT, w1, w2_words, w2_scales, offs, out
                 z_rows = keep.tile([P, PACK, width], BF16, name="z_rows_%d" % i, align_bytes=64)
                 for t in range(PACK):
                     nc.scalar.activation(out=z_rows[:, t, :], in_=rows[:, t, :], func=IDENTITY, bias=minus_mean[:, t : t + 1])
-                nc.vector.tensor_copy(out=z_dst, in_=z_rows[:].rearrange("p t (c i) -> p c t i", i=4))
-            zq = quantise("zq_%d" % i, z[:], width)
+                if route == "both":
+                    nc.vector.tensor_copy(out=z_dst, in_=z_rows[:].rearrange("p t (c i) -> p c t i", i=4))
+                else:
+                    nc.scalar.copy(out=z_dst, in_=z_rows[:].rearrange("p t (c i) -> p c t i", i=4))
+            zq = quantise("zq_%d" % i, z[:], width, "zq_%d" % i)
             acc = psum.tile([P, HALF], F32, name="acc", tag="bank_%d_%d" % (i % PACK, i // PACK))
             nc.tensor.matmul_mx(
                 out=acc[:, 0:width],

@@ -55,14 +55,15 @@ def tile_picked_deepset_none_e_kernel(tc, xT, w1, w2_words, w2_scales, offs, out
                     x_raw[(g, u, i)] = raw
                 if (g, u) == (0, 0):
                     nc.sync.dma_start(offsets[:], offs)
+                    for q in range(4):
+                        nc.sync.dma_start(out=w2_plane[32 * q : 32 * q + 4, :].bitcast(I32), in_=w2_scales[0, 4 * q : 4 * q + 4, :].bitcast(I32))
         w_raw = []
         for g in range(PASSES):
             raw = keep.tile([P, PACK, H], F32, name="w_raw", tag="w_raw_%d" % g, align_bytes=64)
             nc.sync.dma_start(out=raw[:], in_=w_rows[g])
             w_raw.append(raw)
-        nc.sync.dma_start(out=w2_codes[:].bitcast(I32), in_=w2_words[0].rearrange("p n t -> p (n t)").bitcast(I32))
-        for q in range(4):
-            nc.sync.dma_start(out=w2_plane[32 * q : 32 * q + 4, :].bitcast(I32), in_=w2_scales[0, 4 * q : 4 * q + 4, :].bitcast(I32))
+            if g == 0:
+                nc.sync.dma_start(out=w2_codes[:].bitcast(I32), in_=w2_words[0].rearrange("p n t -> p (n t)").bitcast(I32))
 
         def cast(on_vector, dst, src):
             if on_vector:
@@ -149,14 +150,24 @@ def tile_picked_deepset_none_e_kernel(tc, xT, w1, w2_words, w2_scales, offs, out
                 nc.vector.quantize_mx(out=codes[:, cols].bitcast(FP8X4), scales=plane[:, cols], in_=grouped[:, H * t : H * (t + 1)])
             return codes, plane
 
-        grouped = weave(picked1[0], HALF, True, "x_grouped_1_0")
-        xq1 = [quantise("xq_1_0", grouped[:], HALF, "xq_1_0")]
+        for i in range(4):
+            nc.tensor.matmul_mx(
+                out=banks[(PACK - 1, 1)][:],
+                lhsT=w2_codes[:].bitcast(FP8X4),
+                lhsT_scale=w2_plane[:],
+                rhs=xq0[0][0][:].bitcast(FP8X4),
+                rhs_scale=xq0[0][1][:],
+                start=True,
+                stop=True,
+            )
+        grouped = weave(picked1[0], HALF, True, "x_grouped_1")
         wq0 = quantise_weights(0, cast_weights(0))
         for h in range(2):
             product(0, h, xq0[h], slice(0, HALF), wq0)
-        grouped = weave(picked1[1], HALF, True, "w_grouped_0")
-        xq1.append(quantise("xq_1_1", grouped[:], HALF, "xq_1_1"))
+        xq1 = [quantise("xq_1_0", grouped[:], HALF, "w_grouped_0")]
+        grouped = weave(picked1[1], HALF, True, "x_grouped_1")
         wq1 = quantise_weights(1, cast_weights(1))
+        xq1.append(quantise("xq_1_1", grouped[:], HALF, "w_grouped_1"))
 
         sums = keep.tile([P, 2 * PACK], F32, name="sums")
         hidden = [keep.tile([P, PACK * HALF], F32, name="hidden_%d" % h) for h in range(2)]

@@ -21,15 +21,16 @@ P = 128
 PACK = 4
 PASSES = 2
 HALF = 512
+QUARTER = 256
 
-X_CHUNKS = {
-    (0, 0): [(0, 1024, 640), (1024, 1024, 640)],
-    (0, 1): [(0, 1280, 512), (1280, 768, 512)],
-    (1, 0): [(0, 1024, 0), (1024, 1024, 704)],
-    (1, 1): [(0, 768, 0), (768, 512, 0), (1280, 512, 512), (1792, 256, 64)],
-}
-W0_SCALAR_ROWS = 44
+X_CHUNKS = [
+    [(1024, 1024), (1024, 704)],
+    [(1024, 0), (1024, 704)],
+    [(1024, 0), (1024, 704)],
+    [(896, 0), (768, 512), (384, 256)],
+]
 Z_SLICES = [(256, "vector"), (256, "both"), (256, "both"), (128, "scalar"), (128, "vector")]
+EVAC_ON_VECTOR = [[False, False, False, False], [True, True, True, False]]
 
 
 def tile_picked_deepset_none_e_kernel(tc, xT, w1, w2_words, w2_scales, offs, out):
@@ -46,24 +47,28 @@ def tile_picked_deepset_none_e_kernel(tc, xT, w1, w2_words, w2_scales, offs, out
         x_rows = xT.rearrange("(g p j) c -> g p j c", g=PASSES, j=PACK)
         w_rows = w1.rearrange("(g p j) c -> g p j c", g=PASSES, j=PACK)
 
+        w0_raw = keep.tile([P, PACK, H], F32, name="w0_raw", align_bytes=64)
         x_raw = {}
-        for g in range(PASSES):
-            for u in range(2):
-                for i, (c0, width, share) in enumerate(X_CHUNKS[(g, u)]):
-                    raw = keep.tile([P, 2, width], F32, name="x_raw", tag="x_raw_%d_%d_%d" % (g, u, i), align_bytes=64)
-                    nc.sync.dma_start(out=raw[:], in_=x_rows[g][:, 2 * u : 2 * u + 2, c0 : c0 + width])
-                    x_raw[(g, u, i)] = raw
-                if (g, u) == (0, 0):
+        for pair in range(4):
+            g, u = divmod(pair, 2)
+            c0 = 0
+            for i, (width, share) in enumerate(X_CHUNKS[pair]):
+                raw = keep.tile([P, 2, width], F32, name="x_raw", tag="x_raw_%d_%d" % (pair, i), align_bytes=64)
+                nc.sync.dma_start(out=raw[:], in_=x_rows[g][:, 2 * u : 2 * u + 2, c0 : c0 + width])
+                x_raw[(pair, i)] = raw
+                c0 = c0 + width
+                if (pair, i) == (0, 0):
                     nc.sync.dma_start(offsets[:], offs)
-                    for q in range(4):
-                        nc.sync.dma_start(out=w2_plane[32 * q : 32 * q + 4, :].bitcast(I32), in_=w2_scales[0, 4 * q : 4 * q + 4, :].bitcast(I32))
-        w_raw = []
-        for g in range(PASSES):
-            raw = keep.tile([P, PACK, H], F32, name="w_raw", tag="w_raw_%d" % g, align_bytes=64)
-            nc.sync.dma_start(out=raw[:], in_=w_rows[g])
-            w_raw.append(raw)
-            if g == 0:
-                nc.sync.dma_start(out=w2_codes[:].bitcast(I32), in_=w2_words[0].rearrange("p n t -> p (n t)").bitcast(I32))
+            if pair == 1:
+                nc.sync.dma_start(out=w0_raw[:], in_=w_rows[0])
+        w1_raw = []
+        for i in range(2):
+            raw = keep.tile([P, PACK, H // 2], F32, name="w1_raw", tag="w1_raw_%d" % i, align_bytes=64)
+            nc.sync.dma_start(out=raw[:], in_=w_rows[1][:, :, i * (H // 2) : (i + 1) * (H // 2)])
+            w1_raw.append(raw)
+        nc.sync.dma_start(out=w2_codes[:].bitcast(I32), in_=w2_words[0].rearrange("p n t -> p (n t)").bitcast(I32))
+        for q in range(4):
+            nc.sync.dma_start(out=w2_plane[32 * q : 32 * q + 4, :].bitcast(I32), in_=w2_scales[0, 4 * q : 4 * q + 4, :].bitcast(I32))
 
         def cast(on_vector, dst, src):
             if on_vector:
@@ -71,118 +76,133 @@ def tile_picked_deepset_none_e_kernel(tc, xT, w1, w2_words, w2_scales, offs, out
             else:
                 nc.scalar.activation(out=dst, in_=src, func=COPY)
 
-        pairs = keep.tile([P, 4 * 2 * T], BF16, name="pairs", tag="pairs", align_bytes=64)
-
-        def cast_pair(g, u):
-            dst = pairs[:, (2 * g + u) * 2 * T : (2 * g + u + 1) * 2 * T].rearrange("p (c e) -> p c e", e=2)
-            for i, (c0, width, share) in enumerate(X_CHUNKS[(g, u)]):
-                src = x_raw[(g, u, i)][:].rearrange("p e c -> p c e")
+        def cast_pair(pair):
+            window = keep.tile([P, 2 * T], BF16, name="window", tag="window_%d" % pair, align_bytes=64)
+            dst = window[:].rearrange("p (c e) -> p c e", e=2)
+            c0 = 0
+            for i, (width, share) in enumerate(X_CHUNKS[pair]):
+                src = x_raw[(pair, i)][:].rearrange("p e c -> p c e")
                 if share < width:
                     cast(False, dst[:, c0 + share : c0 + width, :], src[:, share:width, :])
                 if share > 0:
                     cast(True, dst[:, c0 : c0 + share, :], src[:, 0:share, :])
+                c0 = c0 + width
+            return window
 
-        def gather(g, u, picked, n0, width):
-            window = pairs[:].bitcast(U32)[:, (2 * g + u) * T : (2 * g + u + 1) * T]
-            nc.vector.tensor_copy(out=picked[:, u, :], in_=window.indirect(offsets[:, n0 // 16 : (n0 + width) // 16]))
+        def gather(window, u, picked, h):
+            nc.vector.tensor_copy(
+                out=picked[:, u, :], in_=window[:].bitcast(U32).indirect(offsets[:, h * HALF // 16 : (h + 1) * HALF // 16])
+            )
 
-        def weave(picked, width, on_vector, tag):
-            grouped = keep.tile([P, PACK * width], BF16, name="x_grouped", tag=tag, align_bytes=64)
+        def weave(on_vector, grouped, picked, n0, width):
             if on_vector:
                 nc.vector.tensor_copy(
-                    out=grouped[:].bitcast(I32).rearrange("p (n u) -> p n u", u=2),
-                    in_=picked[:].bitcast(I32).rearrange("p u n -> p n u"),
+                    out=grouped[:].bitcast(I32).rearrange("p (n u) -> p n u", u=2)[:, n0 : n0 + width, :],
+                    in_=picked[:].bitcast(I32).rearrange("p u n -> p n u")[:, n0 : n0 + width, :],
                 )
             else:
                 nc.scalar.copy(
-                    out=grouped[:].bitcast(U32).rearrange("p (n u) -> p n u", u=2),
-                    in_=picked[:].rearrange("p u n -> p n u"),
+                    out=grouped[:].bitcast(U32).rearrange("p (n u) -> p n u", u=2)[:, n0 : n0 + width, :],
+                    in_=picked[:].rearrange("p u n -> p n u")[:, n0 : n0 + width, :],
                 )
-            return grouped
 
-        def quantise(name, grouped, width, tag):
-            codes = keep.tile([P, width], U32, name="codes", tag=tag, align_bytes=64)
+        def mx_tiles(name, width):
+            codes = keep.tile([P, width], U32, name=name + "_codes", align_bytes=64)
             plane = keep.tile([P, width], U8, name=name + "_plane", align_bytes=64)
-            nc.vector.quantize_mx(out=codes[:].bitcast(FP8X4), scales=plane[:], in_=grouped)
             return codes, plane
+
+        def quantise(mx, grouped, n0, width):
+            nc.vector.quantize_mx(
+                out=mx[0][:, n0 : n0 + width].bitcast(FP8X4), scales=mx[1][:, n0 : n0 + width], in_=grouped[:, PACK * n0 : PACK * (n0 + width)]
+            )
 
         banks = {}
         for h in range(2):
             for t in range(PACK):
                 banks[(t, h)] = psum.tile([P, HALF], F32, name="bank", tag="bank_%d_%d" % (t, h))
 
-        def product(g, h, xq, cols, wq):
+        def product(g, h, xq, wq):
             for t in range(PACK):
                 nc.tensor.matmul_mx(
                     out=banks[(t, h)][:],
-                    lhsT=wq[0][:, t * P : (t + 1) * P].bitcast(FP8X4),
-                    lhsT_scale=wq[1][:, t * P : (t + 1) * P],
-                    rhs=xq[0][:, cols].bitcast(FP8X4),
-                    rhs_scale=xq[1][:, cols],
+                    lhsT=wq[t][0].bitcast(FP8X4),
+                    lhsT_scale=wq[t][1],
+                    rhs=xq[0][:].bitcast(FP8X4),
+                    rhs_scale=xq[1][:],
                     start=(g == 0),
                     stop=(g == PASSES - 1),
                 )
 
         picked0 = [keep.tile([P, 2, HALF], U32, name="picked", tag="picked_0_%d" % h, align_bytes=64) for h in range(2)]
         for u in range(2):
-            cast_pair(0, u)
+            window = cast_pair(u)
             for h in range(2):
-                gather(0, u, picked0[h], h * HALF, HALF)
-        x_grouped = [weave(picked0[h], HALF, h == 1, "x_grouped_0_%d" % h) for h in range(2)]
-        xq0 = [quantise("xq_0_%d" % h, x_grouped[h][:], HALF, "xq_0_%d" % h) for h in range(2)]
+                gather(window, u, picked0[h], h)
+        w0_grouped = keep.tile([P, PACK * H], BF16, name="w0_grouped", align_bytes=64)
+        cast(False, w0_grouped[:].rearrange("p (t m j) -> p m j t", t=PACK, j=PACK), w0_raw[:].rearrange("p j (m t) -> p m j t", t=PACK))
+        xq0 = []
+        grouped0 = []
+        for h in range(2):
+            grouped = keep.tile([P, PACK * HALF], BF16, name="x_grouped", tag="x_grouped_0_%d" % h, align_bytes=64)
+            weave(True, grouped, picked0[h], 0, HALF)
+            grouped0.append(grouped)
+        for h in range(2):
+            xq0.append(mx_tiles("xq0_%d" % h, HALF))
+            quantise(xq0[h], grouped0[h], 0, HALF)
+        wq0_planes = keep.tile([P, P], U8, name="wq0_planes", align_bytes=64)
+        wq0 = []
+
+        def quantise_w0(t, tag):
+            codes = keep.tile([P, P], U32, name="wq0_codes", tag=tag, align_bytes=64)
+            nc.vector.quantize_mx(out=codes[:].bitcast(FP8X4), scales=wq0_planes[4 * t : P, :], in_=w0_grouped[:, t * H : (t + 1) * H])
+            wq0.append((codes[:], wq0_planes[4 * t : P, :]))
+
+        for t in range(PACK - 1):
+            quantise_w0(t, "wq0_codes_%d" % t)
+
+
         picked1 = [keep.tile([P, 2, HALF], U32, name="picked", tag="picked_1_%d" % h, align_bytes=64) for h in range(2)]
         for u in range(2):
-            cast_pair(1, u)
+            window = cast_pair(2 + u)
             for h in range(2):
-                gather(1, u, picked1[h], h * HALF, HALF)
+                gather(window, u, picked1[h], h)
+            if u == 0:
+                quantise_w0(PACK - 1, "window_2")
+                for h in range(2):
+                    product(0, h, xq0[h], wq0)
 
-        def cast_weights(g):
-            grouped = keep.tile([P, PACK * H], BF16, name="w_grouped", tag="w_grouped_%d" % g, align_bytes=64)
-            src = w_raw[g][:].rearrange("p j (m t) -> p m j t", t=PACK)
-            cast(False, grouped[:].rearrange("p (t m j) -> p m j t", t=PACK, j=PACK), src)
-            return grouped
-
-        def quantise_weights(g, grouped):
-            codes = keep.tile([P, H], U32, name="wq_codes_%d" % g, align_bytes=64)
-            plane = keep.tile([P, H], U8, name="wq_plane_%d" % g, align_bytes=64)
-            for t in range(PACK):
-                cols = slice(t * P, (t + 1) * P)
-                nc.vector.quantize_mx(out=codes[:, cols].bitcast(FP8X4), scales=plane[:, cols], in_=grouped[:, H * t : H * (t + 1)])
-            return codes, plane
-
-        for i in range(4):
-            nc.tensor.matmul_mx(
-                out=banks[(PACK - 1, 1)][:],
-                lhsT=w2_codes[:].bitcast(FP8X4),
-                lhsT_scale=w2_plane[:],
-                rhs=xq0[0][0][:].bitcast(FP8X4),
-                rhs_scale=xq0[0][1][:],
-                start=True,
-                stop=True,
-            )
-        grouped = weave(picked1[0], HALF, True, "x_grouped_1")
-        wq0 = quantise_weights(0, cast_weights(0))
-        for h in range(2):
-            product(0, h, xq0[h], slice(0, HALF), wq0)
-        xq1 = [quantise("xq_1_0", grouped[:], HALF, "w_grouped_0")]
-        grouped = weave(picked1[1], HALF, True, "x_grouped_1")
-        wq1 = quantise_weights(1, cast_weights(1))
-        xq1.append(quantise("xq_1_1", grouped[:], HALF, "w_grouped_1"))
+        w1_grouped = keep.tile([P, PACK * H], BF16, name="w1_grouped", align_bytes=64)
+        for i in range(2):
+            dst = w1_grouped[:].rearrange("p (t m j) -> p m j t", t=PACK, j=PACK)[:, i * (P // 2) : (i + 1) * (P // 2)]
+            cast(False, dst, w1_raw[i][:].rearrange("p j (m t) -> p m j t", t=PACK))
+        grouped1 = [keep.tile([P, PACK * HALF], BF16, name="x_grouped", tag="x_grouped_1_0", align_bytes=64)]
+        xq1 = [mx_tiles("xq1_%d" % h, HALF) for h in range(2)]
+        for n0 in (0, QUARTER):
+            weave(True, grouped1[0], picked1[0], n0, QUARTER)
+        for n0 in (0, QUARTER):
+            quantise(xq1[0], grouped1[0], n0, QUARTER)
+        grouped1.append(keep.tile([P, PACK * HALF], BF16, name="x_grouped", tag="w1_raw_1", align_bytes=64))
+        weave(False, grouped1[1], picked1[1], 0, HALF)
+        wq1_mx = mx_tiles("wq1", H)
+        for t in range(PACK):
+            quantise(wq1_mx, w1_grouped, t * P, P)
+        wq1 = [(wq1_mx[0][:, t * P : (t + 1) * P], wq1_mx[1][:, t * P : (t + 1) * P]) for t in range(PACK)]
+        quantise(xq1[1], grouped1[1], 0, HALF)
 
         sums = keep.tile([P, 2 * PACK], F32, name="sums")
         hidden = [keep.tile([P, PACK * HALF], F32, name="hidden_%d" % h) for h in range(2)]
         for h in range(2):
-            product(1, h, xq1[h], slice(0, HALF), wq1)
+            product(1, h, xq1[h], wq1)
             for t in range(PACK):
                 dst = hidden[h][:, t * HALF : (t + 1) * HALF]
                 total = sums[:, h * PACK + t : h * PACK + t + 1]
-                if t % 2 == 0:
+                if EVAC_ON_VECTOR[h][t]:
                     nc.vector.tensor_scalar(out=dst, in0=banks[(t, h)][:], scalar1=1.0, scalar2=None, op0=MULT, op1=ADD, accum_out=total)
                 else:
                     nc.scalar.activation(out=dst, in_=banks[(t, h)][:], func=COPY, accum_out=total)
             if h == 0:
                 first_part = keep.tile([P, PACK], F32, name="first_part")
-                nc.vector.tensor_scalar(out=first_part[:], in0=sums[:, 0:PACK], scalar1=-1.0 / S, scalar2=None, op0=MULT)
+                nc.gpsimd.tensor_scalar(out=first_part[:], in0=sums[:, 0:PACK], scalar1=-1.0 / S, scalar2=0.0, op0=MULT, op1=ADD)
         minus_mean = keep.tile([P, PACK], F32, name="minus_mean")
         for t0, t1 in ((0, PACK - 1), (PACK - 1, PACK)):
             nc.vector.scalar_tensor_tensor(
@@ -210,7 +230,8 @@ def tile_picked_deepset_none_e_kernel(tc, xT, w1, w2_words, w2_scales, offs, out
                     nc.vector.tensor_copy(out=z_dst, in_=z_rows[:].rearrange("p t (c i) -> p c t i", i=4))
                 else:
                     nc.scalar.copy(out=z_dst, in_=z_rows[:].rearrange("p t (c i) -> p c t i", i=4))
-            zq = quantise("zq_%d" % i, z[:], width, "zq_%d" % i)
+            zq = mx_tiles("zq_%d" % i, width)
+            quantise(zq, z, 0, width)
             acc = psum.tile([P, HALF], F32, name="acc", tag="bank_%d_%d" % (i % PACK, i // PACK))
             nc.tensor.matmul_mx(
                 out=acc[:, 0:width],

@@ -89,13 +89,19 @@ def tile_picked_deepset_none_e_kernel(tc, xT, w1, w2_words, w2_scales, offs, out
                 c0 = c0 + width
             return window
 
-        def gather(window, u, picked, h):
+        def gather(window, u, picked, h, n0=0, width=HALF):
+            first = h * HALF + n0
             nc.vector.tensor_copy(
-                out=picked[:, u, :], in_=window[:].bitcast(U32).indirect(offsets[:, h * HALF // 16 : (h + 1) * HALF // 16])
+                out=picked[:, u, n0 : n0 + width], in_=window[:].bitcast(U32).indirect(offsets[:, first // 16 : (first + width) // 16])
             )
 
-        def weave(on_vector, grouped, picked, n0, width):
-            if on_vector:
+        def weave(engine, grouped, picked, n0, width):
+            if engine == "gpsimd":
+                nc.gpsimd.tensor_copy(
+                    out=grouped[:].bitcast(U32).rearrange("p (n u) -> p n u", u=2)[:, n0 : n0 + width, :],
+                    in_=picked[:].rearrange("p u n -> p n u")[:, n0 : n0 + width, :],
+                )
+            elif engine == "vector":
                 nc.vector.tensor_copy(
                     out=grouped[:].bitcast(I32).rearrange("p (n u) -> p n u", u=2)[:, n0 : n0 + width, :],
                     in_=picked[:].bitcast(I32).rearrange("p u n -> p n u")[:, n0 : n0 + width, :],
@@ -144,7 +150,7 @@ def tile_picked_deepset_none_e_kernel(tc, xT, w1, w2_words, w2_scales, offs, out
         grouped0 = []
         for h in range(2):
             grouped = keep.tile([P, PACK * HALF], BF16, name="x_grouped", tag="x_grouped_0_%d" % h, align_bytes=64)
-            weave(True, grouped, picked0[h], 0, HALF)
+            weave("vector", grouped, picked0[h], 0, HALF)
             grouped0.append(grouped)
         for h in range(2):
             xq0.append(mx_tiles("xq0_%d" % h, HALF))
@@ -165,7 +171,11 @@ def tile_picked_deepset_none_e_kernel(tc, xT, w1, w2_words, w2_scales, offs, out
         for u in range(2):
             window = cast_pair(2 + u)
             for h in range(2):
-                gather(window, u, picked1[h], h)
+                if u == 0:
+                    gather(window, u, picked1[h], h)
+                else:
+                    for n0 in (0, QUARTER):
+                        gather(window, u, picked1[h], h, n0, QUARTER)
             if u == 0:
                 quantise_w0(PACK - 1, "window_2")
                 for h in range(2):
@@ -178,16 +188,18 @@ def tile_picked_deepset_none_e_kernel(tc, xT, w1, w2_words, w2_scales, offs, out
         grouped1 = [keep.tile([P, PACK * HALF], BF16, name="x_grouped", tag="x_grouped_1_0", align_bytes=64)]
         xq1 = [mx_tiles("xq1_%d" % h, HALF) for h in range(2)]
         for n0 in (0, QUARTER):
-            weave(True, grouped1[0], picked1[0], n0, QUARTER)
+            weave("gpsimd", grouped1[0], picked1[0], n0, QUARTER)
         for n0 in (0, QUARTER):
             quantise(xq1[0], grouped1[0], n0, QUARTER)
         grouped1.append(keep.tile([P, PACK * HALF], BF16, name="x_grouped", tag="w1_raw_1", align_bytes=64))
-        weave(False, grouped1[1], picked1[1], 0, HALF)
+        for n0 in (0, QUARTER):
+            weave("scalar", grouped1[1], picked1[1], n0, QUARTER)
         wq1_mx = mx_tiles("wq1", H)
         for t in range(PACK):
             quantise(wq1_mx, w1_grouped, t * P, P)
         wq1 = [(wq1_mx[0][:, t * P : (t + 1) * P], wq1_mx[1][:, t * P : (t + 1) * P]) for t in range(PACK)]
-        quantise(xq1[1], grouped1[1], 0, HALF)
+        for n0 in (0, QUARTER):
+            quantise(xq1[1], grouped1[1], n0, QUARTER)
 
         sums = keep.tile([P, 2 * PACK], F32, name="sums")
         hidden = [keep.tile([P, PACK * HALF], F32, name="hidden_%d" % h) for h in range(2)]

@@ -24,12 +24,12 @@ HALF = 512
 QUARTER = 256
 
 X_CHUNKS = [
-    [(1024, 1024), (1024, 704)],
-    [(1024, 0), (1024, 704)],
-    [(1024, 0), (1024, 704)],
-    [(896, 0), (768, 512), (384, 256)],
+    [(2048, 1344, 0)],
+    [(2048, 1344, 0)],
+    [(1024, 0, 0), (1024, 512, 0)],
+    [(1024, 0, 480), (640, 0, 256), (384, 256, 0)],
 ]
-Z_SLICES = [(256, "vector"), (256, "both"), (256, "both"), (128, "scalar"), (128, "vector")]
+Z_SLICES = [(256, "vector"), (256, "both"), (128, "vector"), (128, "both"), (128, "both"), (128, "both")]
 EVAC_ON_VECTOR = [[False, False, False, False], [True, True, True, False]]
 
 
@@ -47,12 +47,12 @@ def tile_picked_deepset_none_e_kernel(tc, xT, w1, w2_words, w2_scales, offs, out
         x_rows = xT.rearrange("(g p j) c -> g p j c", g=PASSES, j=PACK)
         w_rows = w1.rearrange("(g p j) c -> g p j c", g=PASSES, j=PACK)
 
-        w0_raw = keep.tile([P, PACK, H], F32, name="w0_raw", align_bytes=64)
+        w0_raw = keep.tile([P, PACK, H], F32, name="w0_raw", tag="w0_raw", align_bytes=64)
         x_raw = {}
         for pair in range(4):
             g, u = divmod(pair, 2)
             c0 = 0
-            for i, (width, share) in enumerate(X_CHUNKS[pair]):
+            for i, (width, share, third) in enumerate(X_CHUNKS[pair]):
                 raw = keep.tile([P, 2, width], F32, name="x_raw", tag="x_raw_%d_%d" % (pair, i), align_bytes=64)
                 nc.sync.dma_start(out=raw[:], in_=x_rows[g][:, 2 * u : 2 * u + 2, c0 : c0 + width])
                 x_raw[(pair, i)] = raw
@@ -80,12 +80,14 @@ def tile_picked_deepset_none_e_kernel(tc, xT, w1, w2_words, w2_scales, offs, out
             window = keep.tile([P, 2 * T], BF16, name="window", tag="window_%d" % pair, align_bytes=64)
             dst = window[:].rearrange("p (c e) -> p c e", e=2)
             c0 = 0
-            for i, (width, share) in enumerate(X_CHUNKS[pair]):
+            for i, (width, share, third) in enumerate(X_CHUNKS[pair]):
                 src = x_raw[(pair, i)][:].rearrange("p e c -> p c e")
-                if share < width:
-                    cast(False, dst[:, c0 + share : c0 + width, :], src[:, share:width, :])
+                if share + third < width:
+                    cast(False, dst[:, c0 + share + third : c0 + width, :], src[:, share + third : width, :])
                 if share > 0:
                     cast(True, dst[:, c0 : c0 + share, :], src[:, 0:share, :])
+                if third > 0:
+                    nc.gpsimd.tensor_copy(out=dst[:, c0 + share : c0 + share + third, :], in_=src[:, share : share + third, :])
                 c0 = c0 + width
             return window
 
@@ -150,7 +152,7 @@ def tile_picked_deepset_none_e_kernel(tc, xT, w1, w2_words, w2_scales, offs, out
         grouped0 = []
         for h in range(2):
             grouped = keep.tile([P, PACK * HALF], BF16, name="x_grouped", tag="x_grouped_0_%d" % h, align_bytes=64)
-            weave("vector", grouped, picked0[h], 0, HALF)
+            weave(("gpsimd", "vector")[h], grouped, picked0[h], 0, HALF)
             grouped0.append(grouped)
         for h in range(2):
             xq0.append(mx_tiles("xq0_%d" % h, HALF))

@@ -24,13 +24,11 @@ HALF = 512
 QUARTER = 256
 
 X_CHUNKS = [
-    [(2048, 1344, 0)],
-    [(2048, 1344, 0)],
-    [(1024, 0, 0), (1024, 512, 0)],
-    [(1024, 0, 480), (640, 0, 256), (384, 256, 0)],
+    [(1024, 1024, 0), (1024, 704, 0)],
+    [(1024, 0, 0), (1024, 704, 0)],
+    [(1024, 0, 0), (1024, 704, 0)],
+    [(896, 0, 0), (768, 512, 0), (384, 256, 0)],
 ]
-Z_SLICES = [(256, "vector"), (256, "both"), (128, "vector"), (128, "both"), (128, "both"), (128, "both")]
-EVAC_ON_VECTOR = [[False, False, False, False], [True, True, True, False]]
 
 
 def tile_picked_deepset_none_e_kernel(tc, xT, w1, w2_words, w2_scales, offs, out):
@@ -152,7 +150,7 @@ def tile_picked_deepset_none_e_kernel(tc, xT, w1, w2_words, w2_scales, offs, out
         grouped0 = []
         for h in range(2):
             grouped = keep.tile([P, PACK * HALF], BF16, name="x_grouped", tag="x_grouped_0_%d" % h, align_bytes=64)
-            weave(("gpsimd", "vector")[h], grouped, picked0[h], 0, HALF)
+            weave("vector", grouped, picked0[h], 0, HALF)
             grouped0.append(grouped)
         for h in range(2):
             xq0.append(mx_tiles("xq0_%d" % h, HALF))
@@ -203,49 +201,72 @@ def tile_picked_deepset_none_e_kernel(tc, xT, w1, w2_words, w2_scales, offs, out
         for n0 in (0, QUARTER):
             quantise(xq1[1], grouped1[1], n0, QUARTER)
 
-        sums = keep.tile([P, 2 * PACK], F32, name="sums")
+        sums = [
+            keep.tile([P, PACK], F32, name="sums_even"),
+            keep.tile([P, PACK], F32, name="sums_odd", tag="w1_raw_1", align_bytes=64),
+        ]
         hidden = [keep.tile([P, PACK * HALF], F32, name="hidden_%d" % h) for h in range(2)]
+        means = keep.tile([P, PACK, 8], F32, name="means")
         for h in range(2):
             product(1, h, xq1[h], wq1)
             for t in range(PACK):
                 dst = hidden[h][:, t * HALF : (t + 1) * HALF]
-                total = sums[:, h * PACK + t : h * PACK + t + 1]
-                if EVAC_ON_VECTOR[h][t]:
+                col = t // 2 * 2
+                total = sums[t % 2][:, col + h : col + h + 1]
+                if t % 2 == 1:
                     nc.vector.tensor_scalar(out=dst, in0=banks[(t, h)][:], scalar1=1.0, scalar2=None, op0=MULT, op1=ADD, accum_out=total)
                 else:
                     nc.scalar.activation(out=dst, in_=banks[(t, h)][:], func=COPY, accum_out=total)
-            if h == 0:
-                first_part = keep.tile([P, PACK], F32, name="first_part")
-                nc.gpsimd.tensor_scalar(out=first_part[:], in0=sums[:, 0:PACK], scalar1=-1.0 / S, scalar2=0.0, op0=MULT, op1=ADD)
-        minus_mean = keep.tile([P, PACK], F32, name="minus_mean")
-        for t0, t1 in ((0, PACK - 1), (PACK - 1, PACK)):
-            nc.vector.scalar_tensor_tensor(
-                out=minus_mean[:, t0:t1], in0=sums[:, PACK + t0 : PACK + t1], scalar=-1.0 / S, in1=first_part[:, t0:t1], op0=MULT, op1=ADD
-            )
+                if h == 1:
+                    engine = nc.vector if t == PACK - 1 else nc.gpsimd
+                    engine.tensor_scalar(
+                        out=means[:, t, 0:1],
+                        in0=total,
+                        scalar1=sums[t % 2][:, col : col + 1],
+                        scalar2=-1.0 / S,
+                        op0=ADD,
+                        op1=MULT,
+                    )
 
-        c0 = 0
-        for i, (width, route) in enumerate(Z_SLICES):
+        def rows_of(c0, width):
             h, n0 = divmod(c0, HALF)
-            rows = hidden[h][:].rearrange("p (t n) -> p t n", t=PACK)[:, :, n0 : n0 + width]
-            z = keep.tile([P, PACK * width], BF16, name="z_%d" % i, align_bytes=64)
-            z_dst = z[:].rearrange("p (c i t) -> p c t i", i=4, t=PACK)
-            if route == "vector":
-                nc.vector.tensor_tensor(
-                    out=z_dst,
-                    in0=rows.rearrange("p t (c i) -> p c t i", i=4),
-                    in1=minus_mean[:].unsqueeze(1).unsqueeze(3).to_broadcast([P, width // 4, PACK, 4]),
-                    op=ADD,
-                )
+            return hidden[h][:].rearrange("p (t n) -> p t n", t=PACK)[:, :, n0 : n0 + width]
+
+        def z_tile(c0, width):
+            z = keep.tile([P, PACK * width], BF16, name="z_%d" % c0, align_bytes=64)
+            return z, z[:].rearrange("p (c i t) -> p c t i", i=4, t=PACK)
+
+        def centre_rows(c0, width):
+            z_rows = keep.tile([P, PACK, width], BF16, name="z_rows_%d" % c0, align_bytes=64)
+            for t in range(PACK):
+                nc.scalar.activation(out=z_rows[:, t, :], in_=rows_of(c0, width)[:, t, :], func=IDENTITY, bias=means[:, t, 0:1])
+            return z_rows
+
+        def centre_and_interleave(c0, width):
+            z, z_dst = z_tile(c0, width)
+            nc.vector.tensor_tensor(
+                out=z_dst,
+                in0=rows_of(c0, width).rearrange("p t (c i) -> p c t i", i=4),
+                in1=means[:, :, 0:1].unsqueeze(1).to_broadcast([P, width // 4, PACK, 4]),
+                op=ADD,
+            )
+            return z
+
+        def interleave(on_vector, z_rows, n0, c0, width):
+            z, z_dst = z_tile(c0, width)
+            src = z_rows[:, :, n0 : n0 + width].rearrange("p t (c i) -> p c t i", i=4)
+            if on_vector:
+                nc.vector.tensor_copy(out=z_dst, in_=src)
             else:
-                z_rows = keep.tile([P, PACK, width], BF16, name="z_rows_%d" % i, align_bytes=64)
-                for t in range(PACK):
-                    nc.scalar.activation(out=z_rows[:, t, :], in_=rows[:, t, :], func=IDENTITY, bias=minus_mean[:, t : t + 1])
-                if route == "both":
-                    nc.vector.tensor_copy(out=z_dst, in_=z_rows[:].rearrange("p t (c i) -> p c t i", i=4))
-                else:
-                    nc.scalar.copy(out=z_dst, in_=z_rows[:].rearrange("p t (c i) -> p c t i", i=4))
-            zq = mx_tiles("zq_%d" % i, width)
+                nc.scalar.copy(out=z_dst, in_=src)
+            return z
+
+        products = []
+
+        def second_product(z, c0, width):
+            zq = mx_tiles("zq_%d" % c0, width)
             quantise(zq, z, 0, width)
+            i = len(products)
             acc = psum.tile([P, HALF], F32, name="acc", tag="bank_%d_%d" % (i % PACK, i // PACK))
             nc.tensor.matmul_mx(
                 out=acc[:, 0:width],
@@ -256,7 +277,24 @@ def tile_picked_deepset_none_e_kernel(tc, xT, w1, w2_words, w2_scales, offs, out
                 start=True,
                 stop=True,
             )
+            products.append((acc, c0, width))
+
+        rows_b = centre_rows(0, 256)
+        rows_c = centre_rows(256, 256)
+        z_a = centre_and_interleave(512, 256)
+        z_b = interleave(True, rows_b, 0, 0, 256)
+        z_d = interleave(False, centre_rows(896, 128), 0, 896, 128)
+        second_product(z_a, 512, 256)
+        z_e = centre_and_interleave(768, 128)
+        second_product(z_b, 0, 256)
+        z_c = interleave(True, rows_c, 0, 256, 128)
+        second_product(z_e, 768, 128)
+        z_f = interleave(True, rows_c, 128, 384, 128)
+        second_product(z_c, 256, 128)
+        second_product(z_d, 896, 128)
+        second_product(z_f, 384, 128)
+
+        for i, (acc, c0, width) in enumerate(products):
             result = keep.tile([P, width], F32, name="result_%d" % i)
-            cast(i == len(Z_SLICES) - 1, result[:], acc[:, 0:width])
+            cast(i in (5,), result[:], acc[:, 0:width])
             nc.sync.dma_start(out=out[:, c0 : c0 + width], in_=result[:])
-            c0 = c0 + width

@@ -24,10 +24,10 @@ HALF = 512
 QUARTER = 256
 
 X_CHUNKS = [
-    [(1024, 1024, 0), (1024, 704, 0)],
-    [(1024, 0, 0), (1024, 704, 0)],
-    [(1024, 0, 0), (1024, 704, 0)],
-    [(896, 0, 0), (768, 512, 0), (384, 256, 0)],
+    [(2048, 1344, 0)],
+    [(2048, 1344, 0)],
+    [(1024, 0, 0), (1024, 448, 0)],
+    [(1024, 0, 480), (640, 192, 0), (384, 256, 0)],
 ]
 
 

@@ -22,6 +22,8 @@ PACK = 4
 PASSES = 2
 HALF = 512
 QUARTER = 256
+W_CHUNKS = (128, 128, 128, 128)
+LAST_W_TAG = "w1_raw_%d" % (len(W_CHUNKS) - 1)
 
 X_CHUNKS = [
     [(2048, 1344, 0)],
@@ -60,10 +62,12 @@ def tile_picked_deepset_none_e_kernel(tc, xT, w1, w2_words, w2_scales, offs, out
             if pair == 1:
                 nc.sync.dma_start(out=w0_raw[:], in_=w_rows[0])
         w1_raw = []
-        for i in range(2):
-            raw = keep.tile([P, PACK, H // 2], F32, name="w1_raw", tag="w1_raw_%d" % i, align_bytes=64)
-            nc.sync.dma_start(out=raw[:], in_=w_rows[1][:, :, i * (H // 2) : (i + 1) * (H // 2)])
+        c0 = 0
+        for i, width in enumerate(W_CHUNKS):
+            raw = keep.tile([P, PACK, width], F32, name="w1_raw", tag="w1_raw_%d" % i, align_bytes=64)
+            nc.sync.dma_start(out=raw[:], in_=w_rows[1][:, :, c0 : c0 + width])
             w1_raw.append(raw)
+            c0 = c0 + width
         nc.sync.dma_start(out=w2_codes[:].bitcast(I32), in_=w2_words[0].rearrange("p n t -> p (n t)").bitcast(I32))
         for q in range(4):
             nc.sync.dma_start(out=w2_plane[32 * q : 32 * q + 4, :].bitcast(I32), in_=w2_scales[0, 4 * q : 4 * q + 4, :].bitcast(I32))
@@ -182,16 +186,18 @@ def tile_picked_deepset_none_e_kernel(tc, xT, w1, w2_words, w2_scales, offs, out
                     product(0, h, xq0[h], wq0)
 
         w1_grouped = keep.tile([P, PACK * H], BF16, name="w1_grouped", align_bytes=64)
-        for i in range(2):
-            dst = w1_grouped[:].rearrange("p (t m j) -> p m j t", t=PACK, j=PACK)[:, i * (P // 2) : (i + 1) * (P // 2)]
+        m0 = 0
+        for i, width in enumerate(W_CHUNKS):
+            dst = w1_grouped[:].rearrange("p (t m j) -> p m j t", t=PACK, j=PACK)[:, m0 : m0 + width // PACK]
             cast(False, dst, w1_raw[i][:].rearrange("p j (m t) -> p m j t", t=PACK))
+            m0 = m0 + width // PACK
         grouped1 = [keep.tile([P, PACK * HALF], BF16, name="x_grouped", tag="x_grouped_1_0", align_bytes=64)]
         xq1 = [mx_tiles("xq1_%d" % h, HALF) for h in range(2)]
         for n0 in (0, QUARTER):
             weave("gpsimd", grouped1[0], picked1[0], n0, QUARTER)
         for n0 in (0, QUARTER):
             quantise(xq1[0], grouped1[0], n0, QUARTER)
-        grouped1.append(keep.tile([P, PACK * HALF], BF16, name="x_grouped", tag="w1_raw_1", align_bytes=64))
+        grouped1.append(keep.tile([P, PACK * HALF], BF16, name="x_grouped", tag=LAST_W_TAG, align_bytes=64))
         for n0 in (0, QUARTER):
             weave("scalar", grouped1[1], picked1[1], n0, QUARTER)
         wq1_mx = mx_tiles("wq1", H)
@@ -201,32 +207,31 @@ def tile_picked_deepset_none_e_kernel(tc, xT, w1, w2_words, w2_scales, offs, out
         for n0 in (0, QUARTER):
             quantise(xq1[1], grouped1[1], n0, QUARTER)
 
-        sums = [
-            keep.tile([P, PACK], F32, name="sums_even"),
-            keep.tile([P, PACK], F32, name="sums_odd", tag="w1_raw_1", align_bytes=64),
+        first_sums = [
+            keep.tile([P, 2], F32, name="first_even"),
+            keep.tile([P, 2], F32, name="first_odd", tag=LAST_W_TAG, align_bytes=64),
         ]
+        second_sums = keep.tile([P, PACK], F32, name="second_sums")
+        first_part = keep.tile([P, PACK], F32, name="first_part")
+        early_means = keep.tile([P, PACK - 1], F32, name="early_means")
+        means = keep.tile([P, PACK], F32, name="means")
         hidden = [keep.tile([P, PACK * HALF], F32, name="hidden_%d" % h) for h in range(2)]
-        means = keep.tile([P, PACK, 8], F32, name="means")
         for h in range(2):
             product(1, h, xq1[h], wq1)
             for t in range(PACK):
                 dst = hidden[h][:, t * HALF : (t + 1) * HALF]
-                col = t // 2 * 2
-                total = sums[t % 2][:, col + h : col + h + 1]
+                first = first_sums[t % 2][:, t // 2 : t // 2 + 1]
+                total = second_sums[:, t : t + 1] if h == 1 else first
                 if t % 2 == 1:
                     nc.vector.tensor_scalar(out=dst, in0=banks[(t, h)][:], scalar1=1.0, scalar2=None, op0=MULT, op1=ADD, accum_out=total)
                 else:
                     nc.scalar.activation(out=dst, in_=banks[(t, h)][:], func=COPY, accum_out=total)
-                if h == 1:
-                    engine = nc.vector if t == PACK - 1 else nc.gpsimd
-                    engine.tensor_scalar(
-                        out=means[:, t, 0:1],
-                        in0=total,
-                        scalar1=sums[t % 2][:, col : col + 1],
-                        scalar2=-1.0 / S,
-                        op0=ADD,
-                        op1=MULT,
-                    )
+                if h == 1 and t < PACK - 1:
+                    nc.gpsimd.tensor_scalar(out=early_means[:, t : t + 1], in0=total, scalar1=first, scalar2=-1.0 / S, op0=ADD, op1=MULT)
+            if h == 0:
+                for odd in range(2):
+                    nc.gpsimd.tensor_scalar(out=first_part[:, odd:PACK:2], in0=first_sums[odd][:], scalar1=-1.0 / S, scalar2=0.0, op0=MULT, op1=ADD)
+        nc.vector.scalar_tensor_tensor(out=means[:], in0=second_sums[:], scalar=-1.0 / S, in1=first_part[:], op0=MULT, op1=ADD)
 
         def rows_of(c0, width):
             h, n0 = divmod(c0, HALF)
@@ -239,7 +244,7 @@ def tile_picked_deepset_none_e_kernel(tc, xT, w1, w2_words, w2_scales, offs, out
         def centre_rows(c0, width):
             z_rows = keep.tile([P, PACK, width], BF16, name="z_rows_%d" % c0, align_bytes=64)
             for t in range(PACK):
-                nc.scalar.activation(out=z_rows[:, t, :], in_=rows_of(c0, width)[:, t, :], func=IDENTITY, bias=means[:, t, 0:1])
+                nc.scalar.activation(out=z_rows[:, t, :], in_=rows_of(c0, width)[:, t, :], func=IDENTITY, bias=(early_means if t < PACK - 1 else means)[:, t : t + 1])
             return z_rows
 
         def centre_and_interleave(c0, width):
@@ -247,7 +252,7 @@ def tile_picked_deepset_none_e_kernel(tc, xT, w1, w2_words, w2_scales, offs, out
             nc.vector.tensor_tensor(
                 out=z_dst,
                 in0=rows_of(c0, width).rearrange("p t (c i) -> p c t i", i=4),
-                in1=means[:, :, 0:1].unsqueeze(1).to_broadcast([P, width // 4, PACK, 4]),
+                in1=means[:].unsqueeze(1).unsqueeze(3).to_broadcast([P, width // 4, PACK, 4]),
                 op=ADD,
             )
             return z
@@ -296,5 +301,5 @@ def tile_picked_deepset_none_e_kernel(tc, xT, w1, w2_words, w2_scales, offs, out
 
         for i, (acc, c0, width) in enumerate(products):
             result = keep.tile([P, width], F32, name="result_%d" % i)
-            cast(i in (5,), result[:], acc[:, 0:width])
+            cast(i in (2, 3, 5), result[:], acc[:, 0:width])
             nc.sync.dma_start(out=out[:, c0 : c0 + width], in_=result[:])

@@ -28,8 +28,8 @@ LAST_W_TAG = "w1_raw_%d" % (len(W_CHUNKS) - 1)
 X_CHUNKS = [
     [(2048, 1344, 0)],
     [(2048, 1344, 0)],
-    [(1024, 0, 0), (1024, 448, 0)],
-    [(1024, 0, 480), (640, 192, 0), (384, 256, 0)],
+    [(1024, 0, 0), (1024, 0, 0)],
+    [(1024, 256, 192), (640, 192, 0), (384, 256, 0)],
 ]
 
 
@@ -42,7 +42,7 @@ def tile_picked_deepset_none_e_kernel(tc, xT, w1, w2_words, w2_scales, offs, out
         offsets = keep.tile([P, S // 16], U16, name="offsets")
         w2_codes = keep.tile([P, N], U32, name="w2_codes", align_bytes=64)
         w2_plane = keep.tile([P, N], U8, name="w2_plane", align_bytes=64)
-        nc.vector.memset(w2_plane[:].bitcast(I32), 0)
+        nc.gpsimd.memset(w2_plane[:].bitcast(I32), 0)
 
         x_rows = xT.rearrange("(g p j) c -> g p j c", g=PASSES, j=PACK)
         w_rows = w1.rearrange("(g p j) c -> g p j c", g=PASSES, j=PACK)
@@ -59,7 +59,7 @@ def tile_picked_deepset_none_e_kernel(tc, xT, w1, w2_words, w2_scales, offs, out
                 c0 = c0 + width
                 if (pair, i) == (0, 0):
                     nc.sync.dma_start(offsets[:], offs)
-            if pair == 1:
+            if pair == 2:
                 nc.sync.dma_start(out=w0_raw[:], in_=w_rows[0])
         w1_raw = []
         c0 = 0
@@ -148,8 +148,6 @@ def tile_picked_deepset_none_e_kernel(tc, xT, w1, w2_words, w2_scales, offs, out
             window = cast_pair(u)
             for h in range(2):
                 gather(window, u, picked0[h], h)
-        w0_grouped = keep.tile([P, PACK * H], BF16, name="w0_grouped", align_bytes=64)
-        cast(False, w0_grouped[:].rearrange("p (t m j) -> p m j t", t=PACK, j=PACK), w0_raw[:].rearrange("p j (m t) -> p m j t", t=PACK))
         xq0 = []
         grouped0 = []
         for h in range(2):
@@ -167,23 +165,21 @@ def tile_picked_deepset_none_e_kernel(tc, xT, w1, w2_words, w2_scales, offs, out
             nc.vector.quantize_mx(out=codes[:].bitcast(FP8X4), scales=wq0_planes[4 * t : P, :], in_=w0_grouped[:, t * H : (t + 1) * H])
             wq0.append((codes[:], wq0_planes[4 * t : P, :]))
 
+        picked1 = [keep.tile([P, 2, HALF], U32, name="picked", tag="picked_1_%d" % h, align_bytes=64) for h in range(2)]
+        window = cast_pair(2)
+        for h in range(2):
+            gather(window, 0, picked1[h], h)
+        w0_grouped = keep.tile([P, PACK * H], BF16, name="w0_grouped", align_bytes=64)
+        cast(False, w0_grouped[:].rearrange("p (t m j) -> p m j t", t=PACK, j=PACK), w0_raw[:].rearrange("p j (m t) -> p m j t", t=PACK))
         for t in range(PACK - 1):
             quantise_w0(t, "wq0_codes_%d" % t)
-
-
-        picked1 = [keep.tile([P, 2, HALF], U32, name="picked", tag="picked_1_%d" % h, align_bytes=64) for h in range(2)]
-        for u in range(2):
-            window = cast_pair(2 + u)
-            for h in range(2):
-                if u == 0:
-                    gather(window, u, picked1[h], h)
-                else:
-                    for n0 in (0, QUARTER):
-                        gather(window, u, picked1[h], h, n0, QUARTER)
-            if u == 0:
-                quantise_w0(PACK - 1, "window_2")
-                for h in range(2):
-                    product(0, h, xq0[h], wq0)
+        window = cast_pair(3)
+        quantise_w0(PACK - 1, "x_raw_3_0")
+        for h in range(2):
+            product(0, h, xq0[h], wq0)
+        for h in range(2):
+            for n0 in (0, QUARTER):
+                gather(window, 1, picked1[h], h, n0, QUARTER)
 
         w1_grouped = keep.tile([P, PACK * H], BF16, name="w1_grouped", align_bytes=64)
         m0 = 0

@@ -29,7 +29,7 @@ X_CHUNKS = [
     [(2048, 1344, 0)],
     [(2048, 1344, 0)],
     [(1024, 0, 0), (1024, 0, 0)],
-    [(1024, 256, 192), (640, 192, 0), (384, 256, 0)],
+    [(1024, 256, 192), (640, 320, 0), (384, 256, 0)],
 ]
 
 
@@ -197,8 +197,8 @@ def tile_picked_deepset_none_e_kernel(tc, xT, w1, w2_words, w2_scales, offs, out
         for n0 in (0, QUARTER):
             weave("scalar", grouped1[1], picked1[1], n0, QUARTER)
         wq1_mx = mx_tiles("wq1", H)
-        for t in range(PACK):
-            quantise(wq1_mx, w1_grouped, t * P, P)
+        for t in range(0, PACK, 2):
+            quantise(wq1_mx, w1_grouped, t * P, 2 * P)
         wq1 = [(wq1_mx[0][:, t * P : (t + 1) * P], wq1_mx[1][:, t * P : (t + 1) * P]) for t in range(PACK)]
         for n0 in (0, QUARTER):
             quantise(xq1[1], grouped1[1], n0, QUARTER)
@@ -207,54 +207,39 @@ def tile_picked_deepset_none_e_kernel(tc, xT, w1, w2_words, w2_scales, offs, out
             keep.tile([P, 2], F32, name="first_even"),
             keep.tile([P, 2], F32, name="first_odd", tag=LAST_W_TAG, align_bytes=64),
         ]
-        second_sums = keep.tile([P, PACK], F32, name="second_sums")
-        first_part = keep.tile([P, PACK], F32, name="first_part")
-        early_means = keep.tile([P, PACK - 1], F32, name="early_means")
-        means = keep.tile([P, PACK], F32, name="means")
+        second_even = keep.tile([P, 2], F32, name="second_even")
+        shifts = [keep.tile([P, 2], F32, name="shift_even"), keep.tile([P, 2], F32, name="shift_odd")]
         hidden = [keep.tile([P, PACK * HALF], F32, name="hidden_%d" % h) for h in range(2)]
         for h in range(2):
             product(1, h, xq1[h], wq1)
             for t in range(PACK):
                 dst = hidden[h][:, t * HALF : (t + 1) * HALF]
-                first = first_sums[t % 2][:, t // 2 : t // 2 + 1]
-                total = second_sums[:, t : t + 1] if h == 1 else first
+                column = slice(t // 2, t // 2 + 1)
+                first = first_sums[t % 2][:, column]
                 if t % 2 == 1:
-                    nc.vector.tensor_scalar(out=dst, in0=banks[(t, h)][:], scalar1=1.0, scalar2=None, op0=MULT, op1=ADD, accum_out=total)
+                    start, total = (None, first) if h == 0 else (first, shifts[1][:, column])
+                    nc.vector.tensor_scalar(out=dst, in0=banks[(t, h)][:], scalar1=-1.0 / S, scalar2=start, op0=MULT, op1=ADD, accum_out=total)
                 else:
-                    nc.scalar.activation(out=dst, in_=banks[(t, h)][:], func=COPY, accum_out=total)
-                if h == 1 and t < PACK - 1:
-                    nc.gpsimd.tensor_scalar(out=early_means[:, t : t + 1], in0=total, scalar1=first, scalar2=-1.0 / S, op0=ADD, op1=MULT)
-            if h == 0:
-                for odd in range(2):
-                    nc.gpsimd.tensor_scalar(out=first_part[:, odd:PACK:2], in0=first_sums[odd][:], scalar1=-1.0 / S, scalar2=0.0, op0=MULT, op1=ADD)
-        nc.vector.scalar_tensor_tensor(out=means[:], in0=second_sums[:], scalar=-1.0 / S, in1=first_part[:], op0=MULT, op1=ADD)
+                    total = first if h == 0 else second_even[:, column]
+                    nc.scalar.activation(out=dst, in_=banks[(t, h)][:], func=COPY, scale=-1.0 / S, accum_out=total)
+                    if h == 1:
+                        nc.gpsimd.tensor_scalar(out=shifts[0][:, column], in0=total, scalar1=first, scalar2=1.0, op0=ADD, op1=MULT)
 
-        def rows_of(c0, width):
+        def centre_rows(on_vector, c0, width):
             h, n0 = divmod(c0, HALF)
-            return hidden[h][:].rearrange("p (t n) -> p t n", t=PACK)[:, :, n0 : n0 + width]
-
-        def z_tile(c0, width):
-            z = keep.tile([P, PACK * width], BF16, name="z_%d" % c0, align_bytes=64)
-            return z, z[:].rearrange("p (c i t) -> p c t i", i=4, t=PACK)
-
-        def centre_rows(c0, width):
             z_rows = keep.tile([P, PACK, width], BF16, name="z_rows_%d" % c0, align_bytes=64)
             for t in range(PACK):
-                nc.scalar.activation(out=z_rows[:, t, :], in_=rows_of(c0, width)[:, t, :], func=IDENTITY, bias=(early_means if t < PACK - 1 else means)[:, t : t + 1])
+                src = hidden[h][:, t * HALF + n0 : t * HALF + n0 + width]
+                shift = shifts[t % 2][:, t // 2 : t // 2 + 1]
+                if on_vector:
+                    nc.vector.tensor_scalar(out=z_rows[:, t, :], in0=src, scalar1=-1.0 * S, scalar2=shift, op0=MULT, op1=ADD)
+                else:
+                    nc.scalar.activation(out=z_rows[:, t, :], in_=src, func=IDENTITY, scale=-1.0 * S, bias=shift)
             return z_rows
 
-        def centre_and_interleave(c0, width):
-            z, z_dst = z_tile(c0, width)
-            nc.vector.tensor_tensor(
-                out=z_dst,
-                in0=rows_of(c0, width).rearrange("p t (c i) -> p c t i", i=4),
-                in1=means[:].unsqueeze(1).unsqueeze(3).to_broadcast([P, width // 4, PACK, 4]),
-                op=ADD,
-            )
-            return z
-
         def interleave(on_vector, z_rows, n0, c0, width):
-            z, z_dst = z_tile(c0, width)
+            z = keep.tile([P, PACK * width], BF16, name="z_%d" % c0, align_bytes=64)
+            z_dst = z[:].rearrange("p (c i t) -> p c t i", i=4, t=PACK)
             src = z_rows[:, :, n0 : n0 + width].rearrange("p t (c i) -> p c t i", i=4)
             if on_vector:
                 nc.vector.tensor_copy(out=z_dst, in_=src)
@@ -264,9 +249,9 @@ def tile_picked_deepset_none_e_kernel(tc, xT, w1, w2_words, w2_scales, offs, out
 
         products = []
 
-        def second_product(z, c0, width):
+        def second_product(z, z0, c0, width):
             zq = mx_tiles("zq_%d" % c0, width)
-            quantise(zq, z, 0, width)
+            nc.vector.quantize_mx(out=zq[0][:].bitcast(FP8X4), scales=zq[1][:], in_=z[:, PACK * z0 : PACK * (z0 + width)])
             i = len(products)
             acc = psum.tile([P, HALF], F32, name="acc", tag="bank_%d_%d" % (i % PACK, i // PACK))
             nc.tensor.matmul_mx(
@@ -280,20 +265,20 @@ def tile_picked_deepset_none_e_kernel(tc, xT, w1, w2_words, w2_scales, offs, out
             )
             products.append((acc, c0, width))
 
-        rows_b = centre_rows(0, 256)
-        rows_c = centre_rows(256, 256)
-        z_a = centre_and_interleave(512, 256)
+        rows_b = centre_rows(False, 0, 256)
+        rows_c = centre_rows(False, 256, 256)
+        rows_v = centre_rows(True, 512, 384)
         z_b = interleave(True, rows_b, 0, 0, 256)
-        z_d = interleave(False, centre_rows(896, 128), 0, 896, 128)
-        second_product(z_a, 512, 256)
-        z_e = centre_and_interleave(768, 128)
-        second_product(z_b, 0, 256)
+        z_v = interleave(True, rows_v, 0, 512, 384)
+        z_d = interleave(False, centre_rows(False, 896, 128), 0, 896, 128)
+        second_product(z_b, 0, 0, 256)
         z_c = interleave(True, rows_c, 0, 256, 128)
-        second_product(z_e, 768, 128)
+        second_product(z_v, 0, 512, 256)
         z_f = interleave(True, rows_c, 128, 384, 128)
-        second_product(z_c, 256, 128)
-        second_product(z_d, 896, 128)
-        second_product(z_f, 384, 128)
+        second_product(z_v, 256, 768, 128)
+        second_product(z_c, 0, 256, 128)
+        second_product(z_d, 0, 896, 128)
+        second_product(z_f, 0, 384, 128)
 
         for i, (acc, c0, width) in enumerate(products):
             result = keep.tile([P, width], F32, name="result_%d" % i)

@@ -31,6 +31,7 @@ X_CHUNKS = [
     [(1024, 0, 0), (1024, 0, 0)],
     [(1024, 256, 192), (640, 320, 0), (384, 256, 0)],
 ]
+SHARED = 256
 
 
 def tile_picked_deepset_none_e_kernel(tc, xT, w1, w2_words, w2_scales, offs, out):
@@ -197,8 +198,8 @@ def tile_picked_deepset_none_e_kernel(tc, xT, w1, w2_words, w2_scales, offs, out
         for n0 in (0, QUARTER):
             weave("scalar", grouped1[1], picked1[1], n0, QUARTER)
         wq1_mx = mx_tiles("wq1", H)
-        for t in range(0, PACK, 2):
-            quantise(wq1_mx, w1_grouped, t * P, 2 * P)
+        for t in range(PACK):
+            quantise(wq1_mx, w1_grouped, t * P, P)
         wq1 = [(wq1_mx[0][:, t * P : (t + 1) * P], wq1_mx[1][:, t * P : (t + 1) * P]) for t in range(PACK)]
         for n0 in (0, QUARTER):
             quantise(xq1[1], grouped1[1], n0, QUARTER)
@@ -209,11 +210,11 @@ def tile_picked_deepset_none_e_kernel(tc, xT, w1, w2_words, w2_scales, offs, out
         ]
         second_even = keep.tile([P, 2], F32, name="second_even")
         shifts = [keep.tile([P, 2], F32, name="shift_even"), keep.tile([P, 2], F32, name="shift_odd")]
-        hidden = [keep.tile([P, PACK * HALF], F32, name="hidden_%d" % h) for h in range(2)]
+        hidden = keep.tile([P, PACK * S], F32, name="hidden")
         for h in range(2):
             product(1, h, xq1[h], wq1)
             for t in range(PACK):
-                dst = hidden[h][:, t * HALF : (t + 1) * HALF]
+                dst = hidden[:, t * S + h * HALF : t * S + (h + 1) * HALF]
                 column = slice(t // 2, t // 2 + 1)
                 first = first_sums[t % 2][:, column]
                 if t % 2 == 1:
@@ -226,10 +227,9 @@ def tile_picked_deepset_none_e_kernel(tc, xT, w1, w2_words, w2_scales, offs, out
                         nc.gpsimd.tensor_scalar(out=shifts[0][:, column], in0=total, scalar1=first, scalar2=1.0, op0=ADD, op1=MULT)
 
         def centre_rows(on_vector, c0, width):
-            h, n0 = divmod(c0, HALF)
             z_rows = keep.tile([P, PACK, width], BF16, name="z_rows_%d" % c0, align_bytes=64)
             for t in range(PACK):
-                src = hidden[h][:, t * HALF + n0 : t * HALF + n0 + width]
+                src = hidden[:, t * S + c0 : t * S + c0 + width]
                 shift = shifts[t % 2][:, t // 2 : t // 2 + 1]
                 if on_vector:
                     nc.vector.tensor_scalar(out=z_rows[:, t, :], in0=src, scalar1=-1.0 * S, scalar2=shift, op0=MULT, op1=ADD)
@@ -237,15 +237,13 @@ def tile_picked_deepset_none_e_kernel(tc, xT, w1, w2_words, w2_scales, offs, out
                     nc.scalar.activation(out=z_rows[:, t, :], in_=src, func=IDENTITY, scale=-1.0 * S, bias=shift)
             return z_rows
 
-        def interleave(on_vector, z_rows, n0, c0, width):
-            z = keep.tile([P, PACK * width], BF16, name="z_%d" % c0, align_bytes=64)
-            z_dst = z[:].rearrange("p (c i t) -> p c t i", i=4, t=PACK)
+        def interleave(on_vector, z_rows, z, n0, width):
+            z_dst = z[:, PACK * n0 : PACK * (n0 + width)].rearrange("p (c i t) -> p c t i", i=4, t=PACK)
             src = z_rows[:, :, n0 : n0 + width].rearrange("p t (c i) -> p c t i", i=4)
             if on_vector:
                 nc.vector.tensor_copy(out=z_dst, in_=src)
             else:
                 nc.scalar.copy(out=z_dst, in_=src)
-            return z
 
         products = []
 
@@ -265,20 +263,22 @@ def tile_picked_deepset_none_e_kernel(tc, xT, w1, w2_words, w2_scales, offs, out
             )
             products.append((acc, c0, width))
 
+        z_b = keep.tile([P, PACK * 256], BF16, name="z_b", align_bytes=64)
+        z_g = keep.tile([P, PACK * 384], BF16, name="z_g", align_bytes=64)
+        z_v = keep.tile([P, PACK * 384], BF16, name="z_v", align_bytes=64)
         rows_b = centre_rows(False, 0, 256)
-        rows_c = centre_rows(False, 256, 256)
-        rows_v = centre_rows(True, 512, 384)
-        z_b = interleave(True, rows_b, 0, 0, 256)
-        z_v = interleave(True, rows_v, 0, 512, 384)
-        z_d = interleave(False, centre_rows(False, 896, 128), 0, 896, 128)
+        rows_g = centre_rows(False, 256, 384)
+        rows_v = centre_rows(True, 640, 384)
+        interleave(True, rows_b, z_b, 0, 256)
+        interleave(True, rows_v, z_v, 0, 384)
+        interleave(False, rows_g, z_g, SHARED, 384 - SHARED)
         second_product(z_b, 0, 0, 256)
-        z_c = interleave(True, rows_c, 0, 256, 128)
-        second_product(z_v, 0, 512, 256)
-        z_f = interleave(True, rows_c, 128, 384, 128)
-        second_product(z_v, 256, 768, 128)
-        second_product(z_c, 0, 256, 128)
-        second_product(z_d, 0, 896, 128)
-        second_product(z_f, 0, 384, 128)
+        second_product(z_v, 0, 640, 256)
+        interleave(True, rows_g, z_g, 0, SHARED)
+        second_product(z_v, 256, 896, 128)
+        second_product(z_g, 0, 256, 128)
+        second_product(z_g, 128, 384, 128)
+        second_product(z_g, 256, 512, 128)
 
         for i, (acc, c0, width) in enumerate(products):
             result = keep.tile([P, width], F32, name="result_%d" % i)

@@ -31,7 +31,7 @@ X_CHUNKS = [
     [(1024, 0, 0), (1024, 0, 0)],
     [(1024, 256, 192), (640, 320, 0), (384, 256, 0)],
 ]
-SHARED = 256
+SHARED = 192
 
 
 def tile_picked_deepset_none_e_kernel(tc, xT, w1, w2_words, w2_scales, offs, out):

@@ -22,15 +22,8 @@ PACK = 4
 PASSES = 2
 HALF = 512
 QUARTER = 256
-W_CHUNKS = (128, 128, 128, 128)
-LAST_W_TAG = "w1_raw_%d" % (len(W_CHUNKS) - 1)
-
-X_CHUNKS = [
-    [(2048, 1344, 0)],
-    [(2048, 1344, 0)],
-    [(1024, 0, 0), (1024, 0, 0)],
-    [(1024, 256, 192), (640, 320, 0), (384, 256, 0)],
-]
+W0_VECTOR = 96
+W1_VECTOR = 64
 SHARED = 192
 
 
@@ -48,27 +41,17 @@ def tile_picked_deepset_none_e_kernel(tc, xT, w1, w2_words, w2_scales, offs, out
         x_rows = xT.rearrange("(g p j) c -> g p j c", g=PASSES, j=PACK)
         w_rows = w1.rearrange("(g p j) c -> g p j c", g=PASSES, j=PACK)
 
-        w0_raw = keep.tile([P, PACK, H], F32, name="w0_raw", tag="w0_raw", align_bytes=64)
+        w_raw = [keep.tile([P, PACK, H], F32, name="w_raw_%d" % g, align_bytes=64) for g in range(PASSES)]
         x_raw = {}
-        for pair in range(4):
-            g, u = divmod(pair, 2)
-            c0 = 0
-            for i, (width, share, third) in enumerate(X_CHUNKS[pair]):
-                raw = keep.tile([P, 2, width], F32, name="x_raw", tag="x_raw_%d_%d" % (pair, i), align_bytes=64)
-                nc.sync.dma_start(out=raw[:], in_=x_rows[g][:, 2 * u : 2 * u + 2, c0 : c0 + width])
-                x_raw[(pair, i)] = raw
-                c0 = c0 + width
-                if (pair, i) == (0, 0):
+        for g in range(PASSES):
+            for j in range(PACK):
+                if (g, j) == (PASSES - 1, PACK - 1):
+                    nc.sync.dma_start(out=w_raw[0][:], in_=w_rows[0])
+                x_raw[(g, j)] = keep.tile([P, T], F32, name="x_raw_%d_%d" % (g, j), align_bytes=64)
+                nc.sync.dma_start(out=x_raw[(g, j)][:], in_=x_rows[g][:, j, :])
+                if (g, j) == (0, 0):
                     nc.sync.dma_start(offsets[:], offs)
-            if pair == 2:
-                nc.sync.dma_start(out=w0_raw[:], in_=w_rows[0])
-        w1_raw = []
-        c0 = 0
-        for i, width in enumerate(W_CHUNKS):
-            raw = keep.tile([P, PACK, width], F32, name="w1_raw", tag="w1_raw_%d" % i, align_bytes=64)
-            nc.sync.dma_start(out=raw[:], in_=w_rows[1][:, :, c0 : c0 + width])
-            w1_raw.append(raw)
-            c0 = c0 + width
+        nc.sync.dma_start(out=w_raw[1][:], in_=w_rows[1])
         nc.sync.dma_start(out=w2_codes[:].bitcast(I32), in_=w2_words[0].rearrange("p n t -> p (n t)").bitcast(I32))
         for q in range(4):
             nc.sync.dma_start(out=w2_plane[32 * q : 32 * q + 4, :].bitcast(I32), in_=w2_scales[0, 4 * q : 4 * q + 4, :].bitcast(I32))
@@ -79,53 +62,45 @@ def tile_picked_deepset_none_e_kernel(tc, xT, w1, w2_words, w2_scales, offs, out
             else:
                 nc.scalar.activation(out=dst, in_=src, func=COPY)
 
-        def cast_pair(pair):
-            window = keep.tile([P, 2 * T], BF16, name="window", tag="window_%d" % pair, align_bytes=64)
-            dst = window[:].rearrange("p (c e) -> p c e", e=2)
-            c0 = 0
-            for i, (width, share, third) in enumerate(X_CHUNKS[pair]):
-                src = x_raw[(pair, i)][:].rearrange("p e c -> p c e")
-                if share + third < width:
-                    cast(False, dst[:, c0 + share + third : c0 + width, :], src[:, share + third : width, :])
-                if share > 0:
-                    cast(True, dst[:, c0 : c0 + share, :], src[:, 0:share, :])
-                if third > 0:
-                    nc.gpsimd.tensor_copy(out=dst[:, c0 + share : c0 + share + third, :], in_=src[:, share : share + third, :])
-                c0 = c0 + width
-            return window
+        def picked(g, j, first, width):
+            return x_raw[(g, j)][:].indirect(offsets[:, first // 16 : (first + width) // 16])
 
-        def gather(window, u, picked, h, n0=0, width=HALF):
-            first = h * HALF + n0
-            nc.vector.tensor_copy(
-                out=picked[:, u, n0 : n0 + width], in_=window[:].bitcast(U32).indirect(offsets[:, first // 16 : (first + width) // 16])
-            )
+        def slot(grouped, j, n0, width):
+            return grouped[:].rearrange("p (n t) -> p n t", t=PACK)[:, n0 : n0 + width, j]
 
-        def weave(engine, grouped, picked, n0, width):
-            if engine == "gpsimd":
-                nc.gpsimd.tensor_copy(
-                    out=grouped[:].bitcast(U32).rearrange("p (n u) -> p n u", u=2)[:, n0 : n0 + width, :],
-                    in_=picked[:].rearrange("p u n -> p n u")[:, n0 : n0 + width, :],
-                )
-            elif engine == "vector":
-                nc.vector.tensor_copy(
-                    out=grouped[:].bitcast(I32).rearrange("p (n u) -> p n u", u=2)[:, n0 : n0 + width, :],
-                    in_=picked[:].bitcast(I32).rearrange("p u n -> p n u")[:, n0 : n0 + width, :],
-                )
+        def move(engine, dst, src):
+            if engine == "vector":
+                nc.vector.tensor_copy(out=dst, in_=src)
+            elif engine == "gpsimd":
+                nc.gpsimd.tensor_copy(out=dst, in_=src)
             else:
-                nc.scalar.copy(
-                    out=grouped[:].bitcast(U32).rearrange("p (n u) -> p n u", u=2)[:, n0 : n0 + width, :],
-                    in_=picked[:].rearrange("p u n -> p n u")[:, n0 : n0 + width, :],
-                )
+                nc.scalar.copy(out=dst, in_=src)
+
+        def weave(engine, grouped, planes, rows):
+            dst = grouped.rearrange("p (c i t) -> p c t i", i=4, t=PACK)[:, :, 0:rows, :]
+            move(engine, dst, planes[:, 0:rows, :].rearrange("p t (c i) -> p c t i", i=4))
 
         def mx_tiles(name, width):
             codes = keep.tile([P, width], U32, name=name + "_codes", align_bytes=64)
             plane = keep.tile([P, width], U8, name=name + "_plane", align_bytes=64)
             return codes, plane
 
-        def quantise(mx, grouped, n0, width):
-            nc.vector.quantize_mx(
-                out=mx[0][:, n0 : n0 + width].bitcast(FP8X4), scales=mx[1][:, n0 : n0 + width], in_=grouped[:, PACK * n0 : PACK * (n0 + width)]
-            )
+        def quantise(mx, n0, grouped, width):
+            nc.vector.quantize_mx(out=mx[0][:, n0 : n0 + width].bitcast(FP8X4), scales=mx[1][:, n0 : n0 + width], in_=grouped)
+
+        def round_weights(g, on_vector_columns):
+            grouped = keep.tile([P, PACK * H], BF16, name="w_grouped", tag="w_grouped_%d" % g, align_bytes=64)
+            dst = grouped[:].rearrange("p (t m j) -> p m j t", t=PACK, j=PACK)
+            src = w_raw[g][:].rearrange("p j (m t) -> p m j t", t=PACK)
+            cast(False, dst[:, on_vector_columns:P], src[:, on_vector_columns:P])
+            cast(True, dst[:, 0:on_vector_columns], src[:, 0:on_vector_columns])
+            return grouped
+
+        def quantise_weights(g, grouped):
+            mx = mx_tiles("wq%d" % g, H)
+            for t in range(PACK):
+                quantise(mx, t * P, grouped[:, t * H : (t + 1) * H], P)
+            return [(mx[0][:, t * P : (t + 1) * P], mx[1][:, t * P : (t + 1) * P]) for t in range(PACK)]
 
         banks = {}
         for h in range(2):
@@ -144,69 +119,50 @@ def tile_picked_deepset_none_e_kernel(tc, xT, w1, w2_words, w2_scales, offs, out
                     stop=(g == PASSES - 1),
                 )
 
-        picked0 = [keep.tile([P, 2, HALF], U32, name="picked", tag="picked_0_%d" % h, align_bytes=64) for h in range(2)]
-        for u in range(2):
-            window = cast_pair(u)
-            for h in range(2):
-                gather(window, u, picked0[h], h)
-        xq0 = []
-        grouped0 = []
-        for h in range(2):
-            grouped = keep.tile([P, PACK * HALF], BF16, name="x_grouped", tag="x_grouped_0_%d" % h, align_bytes=64)
-            weave("vector", grouped, picked0[h], 0, HALF)
-            grouped0.append(grouped)
-        for h in range(2):
-            xq0.append(mx_tiles("xq0_%d" % h, HALF))
-            quantise(xq0[h], grouped0[h], 0, HALF)
-        wq0_planes = keep.tile([P, P], U8, name="wq0_planes", align_bytes=64)
-        wq0 = []
+        first0 = keep.tile([P, PACK * HALF], BF16, name="first0", align_bytes=64)
+        planes0_wide = keep.tile([P, PACK, HALF], BF16, name="planes0_wide", align_bytes=64)
+        for j in range(PACK):
+            nc.vector.tensor_copy(out=slot(first0, j, 0, HALF), in_=picked(0, j, 0, HALF))
+            nc.scalar.activation(out=planes0_wide[:, j, :], in_=picked(0, j, HALF, HALF), func=COPY)
+        second0 = keep.tile([P, PACK * HALF], BF16, name="second0", align_bytes=64)
+        xq0 = [mx_tiles("xq0_%d" % h, HALF) for h in range(2)]
+        quantise(xq0[0], 0, first0[:], HALF)
 
-        def quantise_w0(t, tag):
-            codes = keep.tile([P, P], U32, name="wq0_codes", tag=tag, align_bytes=64)
-            nc.vector.quantize_mx(out=codes[:].bitcast(FP8X4), scales=wq0_planes[4 * t : P, :], in_=w0_grouped[:, t * H : (t + 1) * H])
-            wq0.append((codes[:], wq0_planes[4 * t : P, :]))
+        first1 = keep.tile([P, PACK * HALF], BF16, name="first1", align_bytes=64)
+        planes1 = keep.tile([P, PACK - 1, HALF], BF16, name="planes1", align_bytes=64)
+        for j in range(PACK - 1):
+            nc.vector.tensor_copy(out=slot(first1, j, 0, HALF), in_=picked(1, j, 0, HALF))
+            if j == 0:
+                weave("scalar", second0[:, 0 : PACK * QUARTER], planes0_wide[:, :, 0:QUARTER], PACK)
+            nc.scalar.activation(out=planes1[:, j, :], in_=picked(1, j, HALF, HALF), func=COPY)
+            if j == 0:
+                weave("scalar", second0[:, PACK * QUARTER : PACK * HALF], planes0_wide[:, :, QUARTER:HALF], PACK)
+            if j == 1:
+                quantise(xq0[1], 0, second0[:], HALF)
+        third1 = keep.tile([P, PACK * QUARTER], BF16, name="third1", align_bytes=64)
+        fourth1 = keep.tile([P, PACK * QUARTER], BF16, name="fourth1", align_bytes=64)
+        weave("gpsimd", third1[:], planes1[:, :, 0:QUARTER], PACK - 1)
+        weave("scalar", fourth1[:], planes1[:, :, QUARTER:HALF], PACK - 1)
 
-        picked1 = [keep.tile([P, 2, HALF], U32, name="picked", tag="picked_1_%d" % h, align_bytes=64) for h in range(2)]
-        window = cast_pair(2)
-        for h in range(2):
-            gather(window, 0, picked1[h], h)
-        w0_grouped = keep.tile([P, PACK * H], BF16, name="w0_grouped", align_bytes=64)
-        cast(False, w0_grouped[:].rearrange("p (t m j) -> p m j t", t=PACK, j=PACK), w0_raw[:].rearrange("p j (m t) -> p m j t", t=PACK))
-        for t in range(PACK - 1):
-            quantise_w0(t, "wq0_codes_%d" % t)
-        window = cast_pair(3)
-        quantise_w0(PACK - 1, "x_raw_3_0")
+        wq0 = quantise_weights(0, round_weights(0, W0_VECTOR))
         for h in range(2):
             product(0, h, xq0[h], wq0)
-        for h in range(2):
-            for n0 in (0, QUARTER):
-                gather(window, 1, picked1[h], h, n0, QUARTER)
 
-        w1_grouped = keep.tile([P, PACK * H], BF16, name="w1_grouped", align_bytes=64)
-        m0 = 0
-        for i, width in enumerate(W_CHUNKS):
-            dst = w1_grouped[:].rearrange("p (t m j) -> p m j t", t=PACK, j=PACK)[:, m0 : m0 + width // PACK]
-            cast(False, dst, w1_raw[i][:].rearrange("p j (m t) -> p m j t", t=PACK))
-            m0 = m0 + width // PACK
-        grouped1 = [keep.tile([P, PACK * HALF], BF16, name="x_grouped", tag="x_grouped_1_0", align_bytes=64)]
+        last = PACK - 1
+        nc.vector.tensor_copy(out=slot(first1, last, 0, HALF), in_=picked(1, last, 0, HALF))
+        for i, (engine, grouped) in enumerate([("gpsimd", third1), ("scalar", fourth1)]):
+            plane = keep.tile([P, QUARTER], BF16, name="last_plane_%d" % i, align_bytes=64)
+            nc.scalar.activation(out=plane[:], in_=picked(1, last, HALF + i * QUARTER, QUARTER), func=COPY)
+            move(engine, slot(grouped, last, 0, QUARTER), plane[:])
         xq1 = [mx_tiles("xq1_%d" % h, HALF) for h in range(2)]
-        for n0 in (0, QUARTER):
-            weave("gpsimd", grouped1[0], picked1[0], n0, QUARTER)
-        for n0 in (0, QUARTER):
-            quantise(xq1[0], grouped1[0], n0, QUARTER)
-        grouped1.append(keep.tile([P, PACK * HALF], BF16, name="x_grouped", tag=LAST_W_TAG, align_bytes=64))
-        for n0 in (0, QUARTER):
-            weave("scalar", grouped1[1], picked1[1], n0, QUARTER)
-        wq1_mx = mx_tiles("wq1", H)
-        for t in range(PACK):
-            quantise(wq1_mx, w1_grouped, t * P, P)
-        wq1 = [(wq1_mx[0][:, t * P : (t + 1) * P], wq1_mx[1][:, t * P : (t + 1) * P]) for t in range(PACK)]
-        for n0 in (0, QUARTER):
-            quantise(xq1[1], grouped1[1], n0, QUARTER)
+        quantise(xq1[0], 0, first1[:], HALF)
+        quantise(xq1[1], 0, third1[:], QUARTER)
+        quantise(xq1[1], QUARTER, fourth1[:], QUARTER)
+        wq1 = quantise_weights(1, round_weights(1, W1_VECTOR))
 
         first_sums = [
             keep.tile([P, 2], F32, name="first_even"),
-            keep.tile([P, 2], F32, name="first_odd", tag=LAST_W_TAG, align_bytes=64),
+            keep.tile([P, 2], F32, name="first_odd", tag="w_grouped_1", align_bytes=64),
         ]
         second_even = keep.tile([P, 2], F32, name="second_even")
         shifts = [keep.tile([P, 2], F32, name="shift_even"), keep.tile([P, 2], F32, name="shift_odd")]

@@ -22,9 +22,10 @@ PACK = 4
 PASSES = 2
 HALF = 512
 QUARTER = 256
-W0_VECTOR = 96
-W1_VECTOR = 64
-SHARED = 192
+W0_VECTOR = 64
+W1_VECTOR = 32
+W1_VECTOR_LATE = 80
+SHARED = 128
 
 
 def tile_picked_deepset_none_e_kernel(tc, xT, w1, w2_words, w2_scales, offs, out):
@@ -88,36 +89,35 @@ def tile_picked_deepset_none_e_kernel(tc, xT, w1, w2_words, w2_scales, offs, out
         def quantise(mx, n0, grouped, width):
             nc.vector.quantize_mx(out=mx[0][:, n0 : n0 + width].bitcast(FP8X4), scales=mx[1][:, n0 : n0 + width], in_=grouped)
 
-        def round_weights(g, on_vector_columns):
-            grouped = keep.tile([P, PACK * H], BF16, name="w_grouped", tag="w_grouped_%d" % g, align_bytes=64)
-            dst = grouped[:].rearrange("p (t m j) -> p m j t", t=PACK, j=PACK)
-            src = w_raw[g][:].rearrange("p j (m t) -> p m j t", t=PACK)
-            cast(False, dst[:, on_vector_columns:P], src[:, on_vector_columns:P])
-            cast(True, dst[:, 0:on_vector_columns], src[:, 0:on_vector_columns])
-            return grouped
+        def round_weights(g, grouped, on_vector, t0, m0, m1):
+            dst = grouped[:].rearrange("p (t m j) -> p m j t", t=2, j=PACK)[:, m0:m1]
+            cast(on_vector, dst, w_raw[g][:].rearrange("p j (m t) -> p m j t", t=PACK)[:, m0:m1, :, t0 : t0 + 2])
 
-        def quantise_weights(g, grouped):
-            mx = mx_tiles("wq%d" % g, H)
-            for t in range(PACK):
-                quantise(mx, t * P, grouped[:, t * H : (t + 1) * H], P)
-            return [(mx[0][:, t * P : (t + 1) * P], mx[1][:, t * P : (t + 1) * P]) for t in range(PACK)]
+        def quantise_weights(name, grouped):
+            mx = mx_tiles(name, 2 * P)
+            quantise(mx, 0, grouped[:], 2 * P)
+            return [(mx[0][:, t * P : (t + 1) * P], mx[1][:, t * P : (t + 1) * P]) for t in range(2)]
+
+        w_grouped = {}
+        for g in range(PASSES):
+            for u in range(2):
+                w_grouped[(g, u)] = keep.tile([P, 2 * H], BF16, name="w_grouped", tag="w_grouped_%d_%d" % (g, u), align_bytes=64)
 
         banks = {}
         for h in range(2):
             for t in range(PACK):
                 banks[(t, h)] = psum.tile([P, HALF], F32, name="bank", tag="bank_%d_%d" % (t, h))
 
-        def product(g, h, xq, wq):
-            for t in range(PACK):
-                nc.tensor.matmul_mx(
-                    out=banks[(t, h)][:],
-                    lhsT=wq[t][0].bitcast(FP8X4),
-                    lhsT_scale=wq[t][1],
-                    rhs=xq[0][:].bitcast(FP8X4),
-                    rhs_scale=xq[1][:],
-                    start=(g == 0),
-                    stop=(g == PASSES - 1),
-                )
+        def product(g, t, h, xq, wq):
+            nc.tensor.matmul_mx(
+                out=banks[(t, h)][:],
+                lhsT=wq[t][0].bitcast(FP8X4),
+                lhsT_scale=wq[t][1],
+                rhs=xq[h][0][:].bitcast(FP8X4),
+                rhs_scale=xq[h][1][:],
+                start=(g == 0),
+                stop=(g == PASSES - 1),
+            )
 
         first0 = keep.tile([P, PACK * HALF], BF16, name="first0", align_bytes=64)
         planes0_wide = keep.tile([P, PACK, HALF], BF16, name="planes0_wide", align_bytes=64)
@@ -144,9 +144,13 @@ def tile_picked_deepset_none_e_kernel(tc, xT, w1, w2_words, w2_scales, offs, out
         weave("gpsimd", third1[:], planes1[:, :, 0:QUARTER], PACK - 1)
         weave("scalar", fourth1[:], planes1[:, :, QUARTER:HALF], PACK - 1)
 
-        wq0 = quantise_weights(0, round_weights(0, W0_VECTOR))
-        for h in range(2):
-            product(0, h, xq0[h], wq0)
+        round_weights(0, w_grouped[(0, 0)], True, 0, 0, P)
+        round_weights(0, w_grouped[(0, 1)], False, 2, W0_VECTOR, P)
+        round_weights(0, w_grouped[(0, 1)], True, 2, 0, W0_VECTOR)
+        wq0 = quantise_weights("wq0_a", w_grouped[(0, 0)]) + quantise_weights("wq0_b", w_grouped[(0, 1)])
+        for t in range(PACK):
+            for h in range(2):
+                product(0, t, h, xq0, wq0)
 
         last = PACK - 1
         nc.vector.tensor_copy(out=slot(first1, last, 0, HALF), in_=picked(1, last, 0, HALF))
@@ -155,43 +159,67 @@ def tile_picked_deepset_none_e_kernel(tc, xT, w1, w2_words, w2_scales, offs, out
             nc.scalar.activation(out=plane[:], in_=picked(1, last, HALF + i * QUARTER, QUARTER), func=COPY)
             move(engine, slot(grouped, last, 0, QUARTER), plane[:])
         xq1 = [mx_tiles("xq1_%d" % h, HALF) for h in range(2)]
-        quantise(xq1[0], 0, first1[:], HALF)
         quantise(xq1[1], 0, third1[:], QUARTER)
+        quantise(xq1[0], 0, first1[:], HALF)
+        round_weights(1, w_grouped[(1, 0)], False, 0, W1_VECTOR, P)
+        round_weights(1, w_grouped[(1, 1)], False, 2, W1_VECTOR_LATE, P)
+        round_weights(1, w_grouped[(1, 0)], True, 0, 0, W1_VECTOR)
         quantise(xq1[1], QUARTER, fourth1[:], QUARTER)
-        wq1 = quantise_weights(1, round_weights(1, W1_VECTOR))
+        wq1 = quantise_weights("wq1_a", w_grouped[(1, 0)])
+        round_weights(1, w_grouped[(1, 1)], True, 2, 0, W1_VECTOR_LATE)
+        wq1 = wq1 + quantise_weights("wq1_b", w_grouped[(1, 1)])
 
-        first_sums = [
-            keep.tile([P, 2], F32, name="first_even"),
-            keep.tile([P, 2], F32, name="first_odd", tag="w_grouped_1", align_bytes=64),
-        ]
-        second_even = keep.tile([P, 2], F32, name="second_even")
-        shifts = [keep.tile([P, 2], F32, name="shift_even"), keep.tile([P, 2], F32, name="shift_odd")]
         hidden = keep.tile([P, PACK * S], F32, name="hidden")
-        for h in range(2):
-            product(1, h, xq1[h], wq1)
-            for t in range(PACK):
-                dst = hidden[:, t * S + h * HALF : t * S + (h + 1) * HALF]
-                column = slice(t // 2, t // 2 + 1)
-                first = first_sums[t % 2][:, column]
-                if t % 2 == 1:
-                    start, total = (None, first) if h == 0 else (first, shifts[1][:, column])
-                    nc.vector.tensor_scalar(out=dst, in0=banks[(t, h)][:], scalar1=-1.0 / S, scalar2=start, op0=MULT, op1=ADD, accum_out=total)
-                else:
-                    total = first if h == 0 else second_even[:, column]
-                    nc.scalar.activation(out=dst, in_=banks[(t, h)][:], func=COPY, scale=-1.0 / S, accum_out=total)
-                    if h == 1:
-                        nc.gpsimd.tensor_scalar(out=shifts[0][:, column], in0=total, scalar1=first, scalar2=1.0, op0=ADD, op1=MULT)
+        order = [(0, 0), (1, 0), (0, 1), (3, 0), (2, 0), (1, 1), (2, 1), (3, 1)]
+        for t, h in order:
+            product(1, t, h, xq1, wq1)
+        sums = {}
+        shifts = {}
 
-        def centre_rows(on_vector, c0, width):
-            z_rows = keep.tile([P, PACK, width], BF16, name="z_rows_%d" % c0, align_bytes=64)
-            for t in range(PACK):
-                src = hidden[:, t * S + c0 : t * S + c0 + width]
-                shift = shifts[t % 2][:, t // 2 : t // 2 + 1]
-                if on_vector:
-                    nc.vector.tensor_scalar(out=z_rows[:, t, :], in0=src, scalar1=-1.0 * S, scalar2=shift, op0=MULT, op1=ADD)
-                else:
-                    nc.scalar.activation(out=z_rows[:, t, :], in_=src, func=IDENTITY, scale=-1.0 * S, bias=shift)
-            return z_rows
+        def empty_bank(t, h, on_vector, start, tag):
+            total = keep.tile([P, 1], F32, name="total", tag=tag, align_bytes=64)
+            dst = hidden[:, t * S + h * HALF : t * S + (h + 1) * HALF]
+            if on_vector:
+                nc.vector.tensor_scalar(out=dst, in0=banks[(t, h)][:], scalar1=-1.0 / S, scalar2=start, op0=MULT, op1=ADD, accum_out=total[:])
+            else:
+                nc.scalar.activation(out=dst, in_=banks[(t, h)][:], func=COPY, scale=-1.0 / S, accum_out=total[:])
+            sums[(t, h)] = total[:]
+
+        def add_sums(on_scalar, t):
+            shift = keep.tile([P, 1], F32, name="shift_%d" % t)
+            if on_scalar:
+                nc.scalar.activation(out=shift[:], in_=sums[(t, 0)], func=IDENTITY, bias=sums[(t, 1)])
+            else:
+                nc.gpsimd.tensor_scalar(out=shift[:], in0=sums[(t, 0)], scalar1=sums[(t, 1)], scalar2=1.0, op0=ADD, op1=MULT)
+            shifts[t] = shift[:]
+
+        groups = [(0, 256), (256, 384), (640, 384)]
+        rows = [keep.tile([P, PACK, width], BF16, name="z_rows", tag="z_rows_%d" % c0, align_bytes=64) for c0, width in groups]
+
+        def centre(engine, i, t):
+            c0, width = groups[i]
+            src = hidden[:, t * S + c0 : t * S + c0 + width]
+            if engine == "scalar":
+                nc.scalar.activation(out=rows[i][:, t, :], in_=src, func=IDENTITY, scale=-1.0 * S, bias=shifts[t])
+            elif engine == "vector":
+                nc.vector.tensor_scalar(out=rows[i][:, t, :], in0=src, scalar1=-1.0 * S, scalar2=shifts[t], op0=MULT, op1=ADD)
+            else:
+                nc.gpsimd.tensor_scalar(out=rows[i][:, t, :], in0=src, scalar1=-1.0 * S, scalar2=shifts[t], op0=MULT, op1=ADD)
+
+        empty_bank(0, 0, False, None, "sum_0_0")
+        empty_bank(1, 0, True, None, "w_grouped_1_1")
+        empty_bank(0, 1, False, None, "sum_0_1")
+        add_sums(False, 0)
+        for i in (2, 0, 1):
+            centre("gpsimd", i, 0)
+        empty_bank(3, 0, True, None, "sum_3_0")
+        empty_bank(2, 0, False, None, "sum_2_0")
+        empty_bank(1, 1, True, sums[(1, 0)], "sum_1_1")
+        shifts[1] = sums[(1, 1)]
+        empty_bank(2, 1, False, None, "sum_2_1")
+        empty_bank(3, 1, True, sums[(3, 0)], "sum_3_1")
+        shifts[3] = sums[(3, 1)]
+        add_sums(True, 2)
 
         def interleave(on_vector, z_rows, z, n0, width):
             z_dst = z[:, PACK * n0 : PACK * (n0 + width)].rearrange("p (c i t) -> p c t i", i=4, t=PACK)
@@ -203,8 +231,11 @@ def tile_picked_deepset_none_e_kernel(tc, xT, w1, w2_words, w2_scales, offs, out
 
         products = []
 
-        def second_product(z, z0, c0, width):
-            zq = mx_tiles("zq_%d" % c0, width)
+        def second_product(z, z0, c0, width, tag):
+            zq = (
+                keep.tile([P, width], U32, name="zq_codes", tag=tag, align_bytes=64),
+                keep.tile([P, width], U8, name="zq_plane_%d" % c0, align_bytes=64),
+            )
             nc.vector.quantize_mx(out=zq[0][:].bitcast(FP8X4), scales=zq[1][:], in_=z[:, PACK * z0 : PACK * (z0 + width)])
             i = len(products)
             acc = psum.tile([P, HALF], F32, name="acc", tag="bank_%d_%d" % (i % PACK, i // PACK))
@@ -219,24 +250,28 @@ def tile_picked_deepset_none_e_kernel(tc, xT, w1, w2_words, w2_scales, offs, out
             )
             products.append((acc, c0, width))
 
-        z_b = keep.tile([P, PACK * 256], BF16, name="z_b", align_bytes=64)
-        z_g = keep.tile([P, PACK * 384], BF16, name="z_g", align_bytes=64)
-        z_v = keep.tile([P, PACK * 384], BF16, name="z_v", align_bytes=64)
-        rows_b = centre_rows(False, 0, 256)
-        rows_g = centre_rows(False, 256, 384)
-        rows_v = centre_rows(True, 640, 384)
-        interleave(True, rows_b, z_b, 0, 256)
-        interleave(True, rows_v, z_v, 0, 384)
-        interleave(False, rows_g, z_g, SHARED, 384 - SHARED)
-        second_product(z_b, 0, 0, 256)
-        second_product(z_v, 0, 640, 256)
-        interleave(True, rows_g, z_g, 0, SHARED)
-        second_product(z_v, 256, 896, 128)
-        second_product(z_g, 0, 256, 128)
-        second_product(z_g, 128, 384, 128)
-        second_product(z_g, 256, 512, 128)
+        centre("scalar", 0, 1)
+        for t in (1, 3, 2):
+            centre("vector", 2, t)
+        centre("scalar", 0, 2)
+        centre("scalar", 0, 3)
+        for t in range(1, PACK):
+            centre("scalar", 1, t)
+        z_own = keep.tile([P, PACK * 384], BF16, name="z_own", tag="z_own", align_bytes=64)
+        interleave(True, rows[2], z_own, 0, 384)
+        z_first = keep.tile([P, PACK * 256], BF16, name="z_first", align_bytes=64)
+        interleave(True, rows[0], z_first, 0, 256)
+        second_product(z_own, 0, 640, 256, "zq_640")
+        second_product(z_first, 0, 0, 256, "zq_0")
+        z_last = keep.tile([P, PACK * 384], BF16, name="z_last", align_bytes=64)
+        interleave(False, rows[1], z_last, SHARED, 384 - SHARED)
+        interleave(True, rows[1], z_last, 0, SHARED)
+        second_product(z_own, 256, 896, 128, "zq_896")
+        second_product(z_last, 0, 256, 128, "zq_256")
+        second_product(z_last, 128, 384, 128, "zq_384")
+        second_product(z_last, 256, 512, 128, "zq_512")
 
         for i, (acc, c0, width) in enumerate(products):
             result = keep.tile([P, width], F32, name="result_%d" % i)
-            cast(i in (2, 3, 5), result[:], acc[:, 0:width])
+            cast(i >= 4, result[:], acc[:, 0:width])
             nc.sync.dma_start(out=out[:, c0 : c0 + width], in_=result[:])

@@ -22,7 +22,7 @@ PACK = 4
 PASSES = 2
 HALF = 512
 QUARTER = 256
-W0_VECTOR = 64
+W0_VECTOR = 32
 W1_VECTOR = 32
 W1_VECTOR_LATE = 80
 SHARED = 128
@@ -114,7 +114,7 @@ def tile_picked_deepset_none_e_kernel(tc, xT, w1, w2_words, w2_scales, offs, out
                 lhsT=wq[t][0].bitcast(FP8X4),
                 lhsT_scale=wq[t][1],
                 rhs=xq[h][0][:].bitcast(FP8X4),
-                rhs_scale=xq[h][1][:],
+                rhs_scale=xq[h][1][:, 0:HALF],
                 start=(g == 0),
                 stop=(g == PASSES - 1),
             )
@@ -125,8 +125,8 @@ def tile_picked_deepset_none_e_kernel(tc, xT, w1, w2_words, w2_scales, offs, out
             nc.vector.tensor_copy(out=slot(first0, j, 0, HALF), in_=picked(0, j, 0, HALF))
             nc.scalar.activation(out=planes0_wide[:, j, :], in_=picked(0, j, HALF, HALF), func=COPY)
         second0 = keep.tile([P, PACK * HALF], BF16, name="second0", align_bytes=64)
-        xq0 = [mx_tiles("xq0_%d" % h, HALF) for h in range(2)]
-        quantise(xq0[0], 0, first0[:], HALF)
+        shared_planes = keep.tile([P, HALF], U8, name="shared_planes", align_bytes=64)
+        xq0_second = (keep.tile([P, HALF], U32, name="xq0_1_codes", align_bytes=64), shared_planes[:])
 
         first1 = keep.tile([P, PACK * HALF], BF16, name="first1", align_bytes=64)
         planes1 = keep.tile([P, PACK - 1, HALF], BF16, name="planes1", align_bytes=64)
@@ -138,7 +138,7 @@ def tile_picked_deepset_none_e_kernel(tc, xT, w1, w2_words, w2_scales, offs, out
             if j == 0:
                 weave("scalar", second0[:, PACK * QUARTER : PACK * HALF], planes0_wide[:, :, QUARTER:HALF], PACK)
             if j == 1:
-                quantise(xq0[1], 0, second0[:], HALF)
+                quantise(xq0_second, 0, second0[:], HALF)
         third1 = keep.tile([P, PACK * QUARTER], BF16, name="third1", align_bytes=64)
         fourth1 = keep.tile([P, PACK * QUARTER], BF16, name="fourth1", align_bytes=64)
         weave("gpsimd", third1[:], planes1[:, :, 0:QUARTER], PACK - 1)
@@ -148,9 +148,14 @@ def tile_picked_deepset_none_e_kernel(tc, xT, w1, w2_words, w2_scales, offs, out
         round_weights(0, w_grouped[(0, 1)], False, 2, W0_VECTOR, P)
         round_weights(0, w_grouped[(0, 1)], True, 2, 0, W0_VECTOR)
         wq0 = quantise_weights("wq0_a", w_grouped[(0, 0)]) + quantise_weights("wq0_b", w_grouped[(0, 1)])
+        xq0_first = (
+            keep.tile([P, HALF], U32, name="xq0_0_codes", tag="w_grouped_0_0", align_bytes=64),
+            keep.tile([P, HALF], U8, name="xq0_0_plane", align_bytes=64),
+        )
+        quantise(xq0_first, 0, first0[:], HALF)
+        xq0 = [xq0_first, xq0_second]
         for t in range(PACK):
-            for h in range(2):
-                product(0, t, h, xq0, wq0)
+            product(0, t, 0, xq0, wq0)
 
         last = PACK - 1
         nc.vector.tensor_copy(out=slot(first1, last, 0, HALF), in_=picked(1, last, 0, HALF))
@@ -158,9 +163,11 @@ def tile_picked_deepset_none_e_kernel(tc, xT, w1, w2_words, w2_scales, offs, out
             plane = keep.tile([P, QUARTER], BF16, name="last_plane_%d" % i, align_bytes=64)
             nc.scalar.activation(out=plane[:], in_=picked(1, last, HALF + i * QUARTER, QUARTER), func=COPY)
             move(engine, slot(grouped, last, 0, QUARTER), plane[:])
-        xq1 = [mx_tiles("xq1_%d" % h, HALF) for h in range(2)]
-        quantise(xq1[1], 0, third1[:], QUARTER)
+        xq1 = [(keep.tile([P, HALF], U32, name="xq1_0_codes", align_bytes=64), shared_planes[4:P, :]), mx_tiles("xq1_1", HALF)]
         quantise(xq1[0], 0, first1[:], HALF)
+        for t in range(PACK):
+            product(0, t, 1, xq0, wq0)
+        quantise(xq1[1], 0, third1[:], QUARTER)
         round_weights(1, w_grouped[(1, 0)], False, 0, W1_VECTOR, P)
         round_weights(1, w_grouped[(1, 1)], False, 2, W1_VECTOR_LATE, P)
         round_weights(1, w_grouped[(1, 0)], True, 0, 0, W1_VECTOR)

@@ -25,7 +25,7 @@ QUARTER = 256
 W0_VECTOR = 32
 W1_VECTOR = 32
 W1_VECTOR_LATE = 80
-SHARED = 128
+SHARED = 192
 
 
 def tile_picked_deepset_none_e_kernel(tc, xT, w1, w2_words, w2_scales, offs, out):
@@ -208,17 +208,13 @@ def tile_picked_deepset_none_e_kernel(tc, xT, w1, w2_words, w2_scales, offs, out
             src = hidden[:, t * S + c0 : t * S + c0 + width]
             if engine == "scalar":
                 nc.scalar.activation(out=rows[i][:, t, :], in_=src, func=IDENTITY, scale=-1.0 * S, bias=shifts[t])
-            elif engine == "vector":
-                nc.vector.tensor_scalar(out=rows[i][:, t, :], in0=src, scalar1=-1.0 * S, scalar2=shifts[t], op0=MULT, op1=ADD)
             else:
-                nc.gpsimd.tensor_scalar(out=rows[i][:, t, :], in0=src, scalar1=-1.0 * S, scalar2=shifts[t], op0=MULT, op1=ADD)
+                nc.vector.tensor_scalar(out=rows[i][:, t, :], in0=src, scalar1=-1.0 * S, scalar2=shifts[t], op0=MULT, op1=ADD)
 
         empty_bank(0, 0, False, None, "sum_0_0")
         empty_bank(1, 0, True, None, "w_grouped_1_1")
         empty_bank(0, 1, False, None, "sum_0_1")
         add_sums(False, 0)
-        for i in (2, 0, 1):
-            centre("gpsimd", i, 0)
         empty_bank(3, 0, True, None, "sum_3_0")
         empty_bank(2, 0, False, None, "sum_2_0")
         empty_bank(1, 1, True, sums[(1, 0)], "sum_1_1")
@@ -257,12 +253,13 @@ def tile_picked_deepset_none_e_kernel(tc, xT, w1, w2_words, w2_scales, offs, out
             )
             products.append((acc, c0, width))
 
+        centre("scalar", 0, 0)
         centre("scalar", 0, 1)
-        for t in (1, 3, 2):
+        for t in (0, 1, 3, 2):
             centre("vector", 2, t)
         centre("scalar", 0, 2)
         centre("scalar", 0, 3)
-        for t in range(1, PACK):
+        for t in range(PACK):
             centre("scalar", 1, t)
         z_own = keep.tile([P, PACK * 384], BF16, name="z_own", tag="z_own", align_bytes=64)
         interleave(True, rows[2], z_own, 0, 384)
@@ -280,5 +277,5 @@ def tile_picked_deepset_none_e_kernel(tc, xT, w1, w2_words, w2_scales, offs, out
 
         for i, (acc, c0, width) in enumerate(products):
             result = keep.tile([P, width], F32, name="result_%d" % i)
-            cast(i >= 4, result[:], acc[:, 0:width])
+            cast(i in (2, 3, 5), result[:], acc[:, 0:width])
             nc.sync.dma_start(out=out[:, c0 : c0 + width], in_=result[:])

@@ -22,7 +22,7 @@ PACK = 4
 PASSES = 2
 HALF = 512
 QUARTER = 256
-W0_VECTOR = 32
+W0_VECTOR = 64
 W1_VECTOR = 32
 W1_VECTOR_LATE = 80
 SHARED = 192
@@ -114,7 +114,7 @@ def tile_picked_deepset_none_e_kernel(tc, xT, w1, w2_words, w2_scales, offs, out
                 lhsT=wq[t][0].bitcast(FP8X4),
                 lhsT_scale=wq[t][1],
                 rhs=xq[h][0][:].bitcast(FP8X4),
-                rhs_scale=xq[h][1][:, 0:HALF],
+                rhs_scale=xq[h][1][:],
                 start=(g == 0),
                 stop=(g == PASSES - 1),
             )
@@ -125,8 +125,8 @@ def tile_picked_deepset_none_e_kernel(tc, xT, w1, w2_words, w2_scales, offs, out
             nc.vector.tensor_copy(out=slot(first0, j, 0, HALF), in_=picked(0, j, 0, HALF))
             nc.scalar.activation(out=planes0_wide[:, j, :], in_=picked(0, j, HALF, HALF), func=COPY)
         second0 = keep.tile([P, PACK * HALF], BF16, name="second0", align_bytes=64)
-        shared_planes = keep.tile([P, HALF], U8, name="shared_planes", align_bytes=64)
-        xq0_second = (keep.tile([P, HALF], U32, name="xq0_1_codes", align_bytes=64), shared_planes[:])
+        xq0 = [mx_tiles("xq0_%d" % h, HALF) for h in range(2)]
+        quantise(xq0[0], 0, first0[:], HALF)
 
         first1 = keep.tile([P, PACK * HALF], BF16, name="first1", align_bytes=64)
         planes1 = keep.tile([P, PACK - 1, HALF], BF16, name="planes1", align_bytes=64)
@@ -138,7 +138,7 @@ def tile_picked_deepset_none_e_kernel(tc, xT, w1, w2_words, w2_scales, offs, out
             if j == 0:
                 weave("scalar", second0[:, PACK * QUARTER : PACK * HALF], planes0_wide[:, :, QUARTER:HALF], PACK)
             if j == 1:
-                quantise(xq0_second, 0, second0[:], HALF)
+                quantise(xq0[1], 0, second0[:], HALF)
         third1 = keep.tile([P, PACK * QUARTER], BF16, name="third1", align_bytes=64)
         fourth1 = keep.tile([P, PACK * QUARTER], BF16, name="fourth1", align_bytes=64)
         weave("gpsimd", third1[:], planes1[:, :, 0:QUARTER], PACK - 1)
@@ -148,14 +148,9 @@ def tile_picked_deepset_none_e_kernel(tc, xT, w1, w2_words, w2_scales, offs, out
         round_weights(0, w_grouped[(0, 1)], False, 2, W0_VECTOR, P)
         round_weights(0, w_grouped[(0, 1)], True, 2, 0, W0_VECTOR)
         wq0 = quantise_weights("wq0_a", w_grouped[(0, 0)]) + quantise_weights("wq0_b", w_grouped[(0, 1)])
-        xq0_first = (
-            keep.tile([P, HALF], U32, name="xq0_0_codes", tag="w_grouped_0_0", align_bytes=64),
-            keep.tile([P, HALF], U8, name="xq0_0_plane", align_bytes=64),
-        )
-        quantise(xq0_first, 0, first0[:], HALF)
-        xq0 = [xq0_first, xq0_second]
         for t in range(PACK):
-            product(0, t, 0, xq0, wq0)
+            for h in range(2):
+                product(0, t, h, xq0, wq0)
 
         last = PACK - 1
         nc.vector.tensor_copy(out=slot(first1, last, 0, HALF), in_=picked(1, last, 0, HALF))
@@ -163,11 +158,9 @@ def tile_picked_deepset_none_e_kernel(tc, xT, w1, w2_words, w2_scales, offs, out
             plane = keep.tile([P, QUARTER], BF16, name="last_plane_%d" % i, align_bytes=64)
             nc.scalar.activation(out=plane[:], in_=picked(1, last, HALF + i * QUARTER, QUARTER), func=COPY)
             move(engine, slot(grouped, last, 0, QUARTER), plane[:])
-        xq1 = [(keep.tile([P, HALF], U32, name="xq1_0_codes", align_bytes=64), shared_planes[4:P, :]), mx_tiles("xq1_1", HALF)]
-        quantise(xq1[0], 0, first1[:], HALF)
-        for t in range(PACK):
-            product(0, t, 1, xq0, wq0)
+        xq1 = [mx_tiles("xq1_%d" % h, HALF) for h in range(2)]
         quantise(xq1[1], 0, third1[:], QUARTER)
+        quantise(xq1[0], 0, first1[:], HALF)
         round_weights(1, w_grouped[(1, 0)], False, 0, W1_VECTOR, P)
         round_weights(1, w_grouped[(1, 1)], False, 2, W1_VECTOR_LATE, P)
         round_weights(1, w_grouped[(1, 0)], True, 0, 0, W1_VECTOR)

@@ -48,7 +48,7 @@ def tile_picked_deepset_none_e_kernel(tc, xT, w1, w2_words, w2_scales, offs, out
             for j in range(PACK):
                 if (g, j) == (PASSES - 1, PACK - 1):
                     nc.sync.dma_start(out=w_raw[0][:], in_=w_rows[0])
-                x_raw[(g, j)] = keep.tile([P, T], F32, name="x_raw_%d_%d" % (g, j), align_bytes=64)
+                x_raw[(g, j)] = keep.tile([P, T], F32, name="x_raw", tag="x_raw_%d_%d" % (g, j), align_bytes=64)
                 nc.sync.dma_start(out=x_raw[(g, j)][:], in_=x_rows[g][:, j, :])
                 if (g, j) == (0, 0):
                     nc.sync.dma_start(offsets[:], offs)
@@ -119,26 +119,32 @@ def tile_picked_deepset_none_e_kernel(tc, xT, w1, w2_words, w2_scales, offs, out
                 stop=(g == PASSES - 1),
             )
 
-        first0 = keep.tile([P, PACK * HALF], BF16, name="first0", align_bytes=64)
+        first0 = keep.tile([P, PACK * HALF], BF16, name="first0", tag="first0", align_bytes=64)
         planes0_wide = keep.tile([P, PACK, HALF], BF16, name="planes0_wide", align_bytes=64)
         for j in range(PACK):
             nc.vector.tensor_copy(out=slot(first0, j, 0, HALF), in_=picked(0, j, 0, HALF))
             nc.scalar.activation(out=planes0_wide[:, j, :], in_=picked(0, j, HALF, HALF), func=COPY)
-        second0 = keep.tile([P, PACK * HALF], BF16, name="second0", align_bytes=64)
-        xq0 = [mx_tiles("xq0_%d" % h, HALF) for h in range(2)]
+        xq0 = [mx_tiles("xq0_0", HALF)]
         quantise(xq0[0], 0, first0[:], HALF)
+        third0 = keep.tile([P, PACK * QUARTER], BF16, name="third0", tag="first0", align_bytes=64)
+        fourth0 = keep.tile([P, PACK * QUARTER], BF16, name="fourth0", align_bytes=64)
+        weave("gpsimd", third0[:], planes0_wide[:, :, 0:QUARTER], PACK)
+        weave("scalar", fourth0[:], planes0_wide[:, :, QUARTER:HALF], PACK)
 
         first1 = keep.tile([P, PACK * HALF], BF16, name="first1", align_bytes=64)
         planes1 = keep.tile([P, PACK - 1, HALF], BF16, name="planes1", align_bytes=64)
         for j in range(PACK - 1):
             nc.vector.tensor_copy(out=slot(first1, j, 0, HALF), in_=picked(1, j, 0, HALF))
-            if j == 0:
-                weave("scalar", second0[:, 0 : PACK * QUARTER], planes0_wide[:, :, 0:QUARTER], PACK)
             nc.scalar.activation(out=planes1[:, j, :], in_=picked(1, j, HALF, HALF), func=COPY)
-            if j == 0:
-                weave("scalar", second0[:, PACK * QUARTER : PACK * HALF], planes0_wide[:, :, QUARTER:HALF], PACK)
             if j == 1:
-                quantise(xq0[1], 0, second0[:], HALF)
+                xq0.append(
+                    (
+                        keep.tile([P, HALF], U32, name="xq0_1_codes", tag="x_raw_1_1", align_bytes=64),
+                        keep.tile([P, HALF], U8, name="xq0_1_plane", align_bytes=64),
+                    )
+                )
+                quantise(xq0[1], QUARTER, fourth0[:], QUARTER)
+                quantise(xq0[1], 0, third0[:], QUARTER)
         third1 = keep.tile([P, PACK * QUARTER], BF16, name="third1", align_bytes=64)
         fourth1 = keep.tile([P, PACK * QUARTER], BF16, name="fourth1", align_bytes=64)
         weave("gpsimd", third1[:], planes1[:, :, 0:QUARTER], PACK - 1)

from contextlib import ExitStack

import concourse.mybir as mybir

K, T, S, H, N = 1024, 2048, 1024, 512, 128
FLOPS = 2 * K * H * S + 2 * H * N * S

F32 = mybir.dt.float32
BF16 = mybir.dt.bfloat16
I32 = mybir.dt.int32
U32 = mybir.dt.uint32
U16 = mybir.dt.uint16
U8 = mybir.dt.uint8
FP8X4 = mybir.dt.float8_e4m3fn_x4
COPY = mybir.ActivationFunctionType.Copy
IDENTITY = mybir.ActivationFunctionType.Identity
ADD = mybir.AluOpType.add
MULT = mybir.AluOpType.mult

P = 128
PACK = 4
PASSES = 2
HALF = 512
QUARTER = 256
W0_VECTOR = 64
W1_VECTOR = 32
W1_VECTOR_LATE = 80
SHARED = 192


def tile_picked_deepset_none_e_kernel(tc, xT, w1, w2_words, w2_scales, offs, out):
    nc = tc.nc
    with ExitStack() as ctx:
        keep = ctx.enter_context(tc.tile_pool(name="keep", bufs=1))
        psum = ctx.enter_context(tc.psum_pool(name="psum", bufs=1))

        offsets = keep.tile([P, S // 16], U16, name="offsets")
        w2_codes = keep.tile([P, N], U32, name="w2_codes", align_bytes=64)
        w2_plane = keep.tile([P, N], U8, name="w2_plane", align_bytes=64)
        nc.gpsimd.memset(w2_plane[:].bitcast(I32), 0)

        x_rows = xT.rearrange("(g p j) c -> g p j c", g=PASSES, j=PACK)
        w_rows = w1.rearrange("(g p j) c -> g p j c", g=PASSES, j=PACK)

        w_raw = [keep.tile([P, PACK, H], F32, name="w_raw_%d" % g, align_bytes=64) for g in range(PASSES)]
        x_raw = {}
        for g in range(PASSES):
            for j in range(PACK):
                if (g, j) == (PASSES - 1, PACK - 1):
                    nc.sync.dma_start(out=w_raw[0][:], in_=w_rows[0])
                x_raw[(g, j)] = keep.tile([P, T], F32, name="x_raw", tag="x_raw_%d_%d" % (g, j), align_bytes=64)
                nc.sync.dma_start(out=x_raw[(g, j)][:], in_=x_rows[g][:, j, :])
                if (g, j) == (0, 0):
                    nc.sync.dma_start(offsets[:], offs)
        nc.sync.dma_start(out=w_raw[1][:], in_=w_rows[1])
        nc.sync.dma_start(out=w2_codes[:].bitcast(I32), in_=w2_words[0].rearrange("p n t -> p (n t)").bitcast(I32))
        for q in range(4):
            nc.sync.dma_start(out=w2_plane[32 * q : 32 * q + 4, :].bitcast(I32), in_=w2_scales[0, 4 * q : 4 * q + 4, :].bitcast(I32))

        def cast(on_vector, dst, src):
            if on_vector:
                nc.vector.tensor_copy(out=dst, in_=src)
            else:
                nc.scalar.activation(out=dst, in_=src, func=COPY)

        def picked(g, j, first, width):
            return x_raw[(g, j)][:].indirect(offsets[:, first // 16 : (first + width) // 16])

        def slot(grouped, j, n0, width):
            return grouped[:].rearrange("p (n t) -> p n t", t=PACK)[:, n0 : n0 + width, j]

        def move(engine, dst, src):
            if engine == "vector":
                nc.vector.tensor_copy(out=dst, in_=src)
            elif engine == "gpsimd":
                nc.gpsimd.tensor_copy(out=dst, in_=src)
            else:
                nc.scalar.copy(out=dst, in_=src)

        def weave(engine, grouped, planes, rows):
            dst = grouped.rearrange("p (c i t) -> p c t i", i=4, t=PACK)[:, :, 0:rows, :]
            move(engine, dst, planes[:, 0:rows, :].rearrange("p t (c i) -> p c t i", i=4))

        def mx_tiles(name, width):
            codes = keep.tile([P, width], U32, name=name + "_codes", align_bytes=64)
            plane = keep.tile([P, width], U8, name=name + "_plane", align_bytes=64)
            return codes, plane

        def quantise(mx, n0, grouped, width):
            nc.vector.quantize_mx(out=mx[0][:, n0 : n0 + width].bitcast(FP8X4), scales=mx[1][:, n0 : n0 + width], in_=grouped)

        def round_weights(g, grouped, on_vector, t0, m0, m1):
            dst = grouped[:].rearrange("p (t m j) -> p m j t", t=2, j=PACK)[:, m0:m1]
            cast(on_vector, dst, w_raw[g][:].rearrange("p j (m t) -> p m j t", t=PACK)[:, m0:m1, :, t0 : t0 + 2])

        def quantise_weights(name, grouped):
            mx = mx_tiles(name, 2 * P)
            quantise(mx, 0, grouped[:], 2 * P)
            return [(mx[0][:, t * P : (t + 1) * P], mx[1][:, t * P : (t + 1) * P]) for t in range(2)]

        w_grouped = {}
        for g in range(PASSES):
            for u in range(2):
                w_grouped[(g, u)] = keep.tile([P, 2 * H], BF16, name="w_grouped", tag="w_grouped_%d_%d" % (g, u), align_bytes=64)

        banks = {}
        for h in range(2):
            for t in range(PACK):
                banks[(t, h)] = psum.tile([P, HALF], F32, name="bank", tag="bank_%d_%d" % (t, h))

        def product(g, t, h, xq, wq):
            nc.tensor.matmul_mx(
                out=banks[(t, h)][:],
                lhsT=wq[t][0].bitcast(FP8X4),
                lhsT_scale=wq[t][1],
                rhs=xq[h][0][:].bitcast(FP8X4),
                rhs_scale=xq[h][1][:],
                start=(g == 0),
                stop=(g == PASSES - 1),
            )

        first0 = keep.tile([P, PACK * HALF], BF16, name="first0", tag="first0", align_bytes=64)
        planes0_wide = keep.tile([P, PACK, HALF], BF16, name="planes0_wide", align_bytes=64)
        for j in range(PACK):
            nc.vector.tensor_copy(out=slot(first0, j, 0, HALF), in_=picked(0, j, 0, HALF))
            nc.scalar.activation(out=planes0_wide[:, j, :], in_=picked(0, j, HALF, HALF), func=COPY)
        xq0 = [mx_tiles("xq0_0", HALF)]
        quantise(xq0[0], 0, first0[:], HALF)
        third0 = keep.tile([P, PACK * QUARTER], BF16, name="third0", tag="first0", align_bytes=64)
        fourth0 = keep.tile([P, PACK * QUARTER], BF16, name="fourth0", align_bytes=64)
        weave("gpsimd", third0[:], planes0_wide[:, :, 0:QUARTER], PACK)
        weave("scalar", fourth0[:], planes0_wide[:, :, QUARTER:HALF], PACK)

        first1 = keep.tile([P, PACK * HALF], BF16, name="first1", align_bytes=64)
        planes1 = keep.tile([P, PACK - 1, HALF], BF16, name="planes1", align_bytes=64)
        for j in range(PACK - 1):
            nc.vector.tensor_copy(out=slot(first1, j, 0, HALF), in_=picked(1, j, 0, HALF))
            nc.scalar.activation(out=planes1[:, j, :], in_=picked(1, j, HALF, HALF), func=COPY)
            if j == 1:
                xq0.append(
                    (
                        keep.tile([P, HALF], U32, name="xq0_1_codes", tag="x_raw_1_1", align_bytes=64),
                        keep.tile([P, HALF], U8, name="xq0_1_plane", align_bytes=64),
                    )
                )
                quantise(xq0[1], QUARTER, fourth0[:], QUARTER)
                quantise(xq0[1], 0, third0[:], QUARTER)
        third1 = keep.tile([P, PACK * QUARTER], BF16, name="third1", align_bytes=64)
        fourth1 = keep.tile([P, PACK * QUARTER], BF16, name="fourth1", align_bytes=64)
        weave("gpsimd", third1[:], planes1[:, :, 0:QUARTER], PACK - 1)
        weave("scalar", fourth1[:], planes1[:, :, QUARTER:HALF], PACK - 1)

        round_weights(0, w_grouped[(0, 0)], True, 0, 0, P)
        round_weights(0, w_grouped[(0, 1)], False, 2, W0_VECTOR, P)
        round_weights(0, w_grouped[(0, 1)], True, 2, 0, W0_VECTOR)
        wq0 = quantise_weights("wq0_a", w_grouped[(0, 0)]) + quantise_weights("wq0_b", w_grouped[(0, 1)])
        for t in range(PACK):
            for h in range(2):
                product(0, t, h, xq0, wq0)

        last = PACK - 1
        nc.vector.tensor_copy(out=slot(first1, last, 0, HALF), in_=picked(1, last, 0, HALF))
        for i, (engine, grouped) in enumerate([("gpsimd", third1), ("scalar", fourth1)]):
            plane = keep.tile([P, QUARTER], BF16, name="last_plane_%d" % i, align_bytes=64)
            nc.scalar.activation(out=plane[:], in_=picked(1, last, HALF + i * QUARTER, QUARTER), func=COPY)
            move(engine, slot(grouped, last, 0, QUARTER), plane[:])
        xq1 = [mx_tiles("xq1_%d" % h, HALF) for h in range(2)]
        quantise(xq1[1], 0, third1[:], QUARTER)
        quantise(xq1[0], 0, first1[:], HALF)
        round_weights(1, w_grouped[(1, 0)], False, 0, W1_VECTOR, P)
        round_weights(1, w_grouped[(1, 1)], False, 2, W1_VECTOR_LATE, P)
        round_weights(1, w_grouped[(1, 0)], True, 0, 0, W1_VECTOR)
        quantise(xq1[1], QUARTER, fourth1[:], QUARTER)
        wq1 = quantise_weights("wq1_a", w_grouped[(1, 0)])
        round_weights(1, w_grouped[(1, 1)], True, 2, 0, W1_VECTOR_LATE)
        wq1 = wq1 + quantise_weights("wq1_b", w_grouped[(1, 1)])

        hidden = keep.tile([P, PACK * S], F32, name="hidden")
        order = [(0, 0), (1, 0), (0, 1), (3, 0), (2, 0), (1, 1), (2, 1), (3, 1)]
        for t, h in order:
            product(1, t, h, xq1, wq1)
        sums = {}
        shifts = {}

        def empty_bank(t, h, on_vector, start, tag):
            total = keep.tile([P, 1], F32, name="total", tag=tag, align_bytes=64)
            dst = hidden[:, t * S + h * HALF : t * S + (h + 1) * HALF]
            if on_vector:
                nc.vector.tensor_scalar(out=dst, in0=banks[(t, h)][:], scalar1=-1.0 / S, scalar2=start, op0=MULT, op1=ADD, accum_out=total[:])
            else:
                nc.scalar.activation(out=dst, in_=banks[(t, h)][:], func=COPY, scale=-1.0 / S, accum_out=total[:])
            sums[(t, h)] = total[:]

        def add_sums(on_scalar, t):
            shift = keep.tile([P, 1], F32, name="shift_%d" % t)
            if on_scalar:
                nc.scalar.activation(out=shift[:], in_=sums[(t, 0)], func=IDENTITY, bias=sums[(t, 1)])
            else:
                nc.gpsimd.tensor_scalar(out=shift[:], in0=sums[(t, 0)], scalar1=sums[(t, 1)], scalar2=1.0, op0=ADD, op1=MULT)
            shifts[t] = shift[:]

        groups = [(0, 256), (256, 384), (640, 384)]
        rows = [keep.tile([P, PACK, width], BF16, name="z_rows", tag="z_rows_%d" % c0, align_bytes=64) for c0, width in groups]

        def centre(engine, i, t):
            c0, width = groups[i]
            src = hidden[:, t * S + c0 : t * S + c0 + width]
            if engine == "scalar":
                nc.scalar.activation(out=rows[i][:, t, :], in_=src, func=IDENTITY, scale=-1.0 * S, bias=shifts[t])
            else:
                nc.vector.tensor_scalar(out=rows[i][:, t, :], in0=src, scalar1=-1.0 * S, scalar2=shifts[t], op0=MULT, op1=ADD)

        empty_bank(0, 0, False, None, "sum_0_0")
        empty_bank(1, 0, True, None, "w_grouped_1_1")
        empty_bank(0, 1, False, None, "sum_0_1")
        add_sums(False, 0)
        empty_bank(3, 0, True, None, "sum_3_0")
        empty_bank(2, 0, False, None, "sum_2_0")
        empty_bank(1, 1, True, sums[(1, 0)], "sum_1_1")
        shifts[1] = sums[(1, 1)]
        empty_bank(2, 1, False, None, "sum_2_1")
        empty_bank(3, 1, True, sums[(3, 0)], "sum_3_1")
        shifts[3] = sums[(3, 1)]
        add_sums(True, 2)

        def interleave(on_vector, z_rows, z, n0, width):
            z_dst = z[:, PACK * n0 : PACK * (n0 + width)].rearrange("p (c i t) -> p c t i", i=4, t=PACK)
            src = z_rows[:, :, n0 : n0 + width].rearrange("p t (c i) -> p c t i", i=4)
            if on_vector:
                nc.vector.tensor_copy(out=z_dst, in_=src)
            else:
                nc.scalar.copy(out=z_dst, in_=src)

        products = []

        def second_product(z, z0, c0, width, tag):
            zq = (
                keep.tile([P, width], U32, name="zq_codes", tag=tag, align_bytes=64),
                keep.tile([P, width], U8, name="zq_plane_%d" % c0, align_bytes=64),
            )
            nc.vector.quantize_mx(out=zq[0][:].bitcast(FP8X4), scales=zq[1][:], in_=z[:, PACK * z0 : PACK * (z0 + width)])
            i = len(products)
            acc = psum.tile([P, HALF], F32, name="acc", tag="bank_%d_%d" % (i % PACK, i // PACK))
            nc.tensor.matmul_mx(
                out=acc[:, 0:width],
                lhsT=w2_codes[:].bitcast(FP8X4),
                lhsT_scale=w2_plane[:],
                rhs=zq[0][:].bitcast(FP8X4),
                rhs_scale=zq[1][:],
                start=True,
                stop=True,
            )
            products.append((acc, c0, width))

        centre("scalar", 0, 0)
        centre("scalar", 0, 1)
        for t in (0, 1, 3, 2):
            centre("vector", 2, t)
        centre("scalar", 0, 2)
        centre("scalar", 0, 3)
        for t in range(PACK):
            centre("scalar", 1, t)
        z_own = keep.tile([P, PACK * 384], BF16, name="z_own", tag="z_own", align_bytes=64)
        interleave(True, rows[2], z_own, 0, 384)
        z_first = keep.tile([P, PACK * 256], BF16, name="z_first", align_bytes=64)
        interleave(True, rows[0], z_first, 0, 256)
        second_product(z_own, 0, 640, 256, "zq_640")
        second_product(z_first, 0, 0, 256, "zq_0")
        z_last = keep.tile([P, PACK * 384], BF16, name="z_last", align_bytes=64)
        interleave(False, rows[1], z_last, SHARED, 384 - SHARED)
        interleave(True, rows[1], z_last, 0, SHARED)
        second_product(z_own, 256, 896, 128, "zq_896")
        second_product(z_last, 0, 256, 128, "zq_256")
        second_product(z_last, 128, 384, 128, "zq_384")
        second_product(z_last, 256, 512, 128, "zq_512")

        for i, (acc, c0, width) in enumerate(products):
            result = keep.tile([P, width], F32, name="result_%d" % i)
            cast(i in (2, 3, 5), result[:], acc[:, 0:width])
            nc.sync.dma_start(out=out[:, c0 : c0 + width], in_=result[:])
